import numpy as np
import ml_dtypes


def mxq(x, axis, fmt="e4m3"):
    dtype, down = {"e4m3": (ml_dtypes.float8_e4m3fn, 7), "e5m2": (ml_dtypes.float8_e5m2, 14)}[fmt]
    v = np.moveaxis(np.asarray(x, np.float32).astype(ml_dtypes.bfloat16).astype(np.float64), axis, -1)
    blocks = v.reshape(v.shape[:-1] + (-1, 32))
    amax = np.abs(blocks).max(-1, keepdims=True)
    byte = np.maximum(np.where(amax > 0, np.frexp(amax)[1] - 1 + 127, 0) - down, 1)
    scale = np.exp2(byte - 127.0)
    codes = (blocks / scale).astype(np.float32).astype(dtype).astype(np.float64)
    return np.moveaxis((codes * scale).reshape(v.shape), -1, axis)


WIDE = False


def mx_kscale(k):
    if not WIDE:
        return np.ones(k)
    levels = np.array([10, -10, 5, -5, 0])
    if k % 512:
        return np.exp2(np.random.permutation(np.resize(levels, k // 32))).repeat(32)
    a = np.empty((k // 512, 16))
    for p in range(k // 512):
        a[p, :8] = np.random.permutation(np.resize(levels, 8))
        for g in range(8):
            far = levels[np.abs(levels - a[p, g]) >= 10]
            a[p, g + 8] = far[np.random.randint(len(far))]
    return np.exp2(a.ravel()).repeat(32)


def f64(x):
    return np.asarray(x).astype(np.float64)


def striped(idx):
    return np.tile(idx.reshape(-1, 16).T, (8, 1)).astype(np.uint16)


def unstriped(offs):
    return offs[:16].T.reshape(-1).astype(np.int64)


E2M1 = np.array([0.0, 0.5, 1.0, 1.5, 2.0, 3.0, 4.0, 6.0, -0.0, -0.5, -1.0, -1.5, -2.0, -3.0, -4.0, -6.0])


def pack_weight(w, fmt):
    k, n = w.shape
    w = f64(np.asarray(w, np.float32).astype(ml_dtypes.bfloat16)).reshape(k // 32, 32, n)
    amax = np.abs(w).max(1)
    if fmt == "e4m3":
        byte = np.frexp(amax)[1] - 1 + 127 - 7
    else:
        mant, ex = np.frexp(amax / 6.0)
        byte = np.where(mant > 0.5, ex, ex - 1) + 127
    byte = np.clip(np.where(amax > 0, byte, 1), 1, 254)
    scaled = (w * np.exp2(127.0 - byte)[:, None, :]).reshape(k, n).astype(np.float32)
    by_word = np.ascontiguousarray(scaled.reshape(k // 512, 128, 4, n).transpose(0, 1, 3, 2))
    if fmt == "e4m3":
        words = by_word.astype(ml_dtypes.float8_e4m3fn).view(np.uint8)
    else:
        c = by_word.astype(ml_dtypes.float4_e2m1fn).view(np.uint8) & 0xF
        words = (c[..., 0::2] | (c[..., 1::2] << 4)).reshape(k // 512, 128, 2 * n)
    return np.ascontiguousarray(words), np.ascontiguousarray(byte.astype(np.uint8).reshape(k // 512, 16, n))


def unpack_weight(words, scales, fmt):
    g, _, n = scales.shape
    words = np.ascontiguousarray(words).reshape(g, 128, n, -1)
    if fmt == "e4m3":
        vals = words.view(ml_dtypes.float8_e4m3fn).astype(np.float64)
    else:
        nib = np.empty((g, 128, n, 4), np.uint8)
        nib[..., 0::2] = words & 0xF
        nib[..., 1::2] = words >> 4
        vals = E2M1[nib]
    vals = vals * np.repeat(np.exp2(scales.astype(np.float64) - 127.0), 8, axis=1)[..., None]
    return vals.transpose(0, 1, 3, 2).reshape(g * 512, n)


def gelu(v):
    return 0.5 * v * (1.0 + np.tanh(np.sqrt(2.0 / np.pi) * (v + 0.044715 * v**3)))


K, H, T, S, T2, P = 512, 1024, 4096, 1024, 2048, 512

def setup_inputs():
    n = np.random.standard_normal
    s = mx_kscale(K)[:, None]
    u = mx_kscale(H)[:, None]
    d = {}
    d["tab_words"], d["tab_scales"] = pack_weight(n((K, T)) * s, "e4m3")
    d["offs"] = striped(np.random.permutation(T)[:S])
    d["offs2"] = striped(np.random.permutation(T2)[:S])
    d["offs3"] = striped(np.random.permutation(T2)[:P])
    d["offs4"] = striped(np.random.permutation(T2)[:P])
    d["w1"] = (0.25 * n((K, H)) / s / K ** 0.5).astype(np.float32)
    d["w2_words"], d["w2_scales"] = pack_weight(1.5 * n((K, H)) / s / K ** 0.5, "e2m1")
    d["w3"] = (0.52 * n((K, H)) / s / K ** 0.5).astype(np.float32)
    d["wgs"] = np.exp(0.3 * n((128, S))).astype(np.float32)
    d["page0"] = (0.5 * n((H, T2))).astype(np.float32)
    d["gs"] = (1.8 * np.exp(0.3 * n(H)) * u[:, 0]).astype(np.float32)
    d["w4"] = (0.8 * n((H, H)) / u / u.T / H ** 0.5).astype(np.float32)
    d["w5_words"], d["w5_scales"] = pack_weight(-0.4 * n((H, H)) / u ** 2 / u.T / H ** 0.5, "e2m1")
    return d

def reference(tab_words, tab_scales, offs, offs2, offs3, offs4, w1, w2_words, w2_scales, w3, wgs, page0, gs, w4, w5_words, w5_scales):
    v = unpack_weight(tab_words, tab_scales, "e4m3")[:, unstriped(offs)]
    f = mxq(f64(w1), 0, "e4m3").T @ v
    b = unpack_weight(w2_words, w2_scales, "e2m1").T @ v
    d = mxq(f64(w3), 0, "e4m3").T @ v
    h = np.tanh(b) * np.sin(d) + f
    page = f64(page0).copy()
    page[:, unstriped(offs2)] = np.tile(f64(wgs), (H // 128, 1)) * h
    page = f64(gs)[:, None] * page
    x = page[:, unstriped(offs3)]
    xx = np.square(x)
    y = (mxq(f64(w4), 0, "e4m3").T @ mxq(x, 0, "e4m3")
              + unpack_weight(w5_words, w5_scales, "e2m1").T @ mxq(xx, 0, "e4m3"))
    return y * page[:, unstriped(offs4)]

@@ -1,0 +1,322 @@
+import math
+from contextlib import ExitStack
+
+import concourse.mybir as mybir
+from concourse.masks import make_identity
+
+K, H, T, S, T2, M = 512, 1024, 4096, 1024, 2048, 512
+FLOPS = 2 * (3 * K * H * S + 2 * H * H * M)
+
+F32 = mybir.dt.float32
+BF16 = mybir.dt.bfloat16
+I32 = mybir.dt.int32
+U32 = mybir.dt.uint32
+U16 = mybir.dt.uint16
+U8 = mybir.dt.uint8
+FP8X4 = mybir.dt.float8_e4m3fn_x4
+FP4X4 = mybir.dt.float4_e2m1fn_x4
+ACT = mybir.ActivationFunctionType
+MULT = mybir.AluOpType.mult
+ADD = mybir.AluOpType.add
+
+P = 128
+PACK = 4
+HALF = P * PACK
+ROUNDER = 1.5 * 2.0**23
+
+
+def tile_list_digester_layer_features_kernel(
+    tc, tab_words, tab_scales, offs, offs2, offs3, offs4, w1, w2_words, w2_scales, w3, wgs, page0, gs, w4,
+    w5_words, w5_scales, out,
+):
+    nc = tc.nc
+    with ExitStack() as ctx:
+        lists = ctx.enter_context(tc.tile_pool(name="lists", bufs=1))
+        sb = ctx.enter_context(tc.tile_pool(name="sb", bufs=1))
+        psum = ctx.enter_context(tc.psum_pool(name="psum", bufs=2))
+
+        def sbuf(shape, dtype, tag, bufs=1):
+            return sb.tile(shape, dtype, name=tag, tag=tag, bufs=bufs, align_bytes=64)
+
+        def bank(tag):
+            return psum.tile([P, HALF], F32, name=tag, tag=tag)
+
+        def load_list(src, name):
+            tile = lists.tile([P, src.shape[1]], U16, name=name)
+            nc.sync.dma_start(tile[:], src)
+            return tile
+
+        def load_scale_rows(engine, plane, rows):
+            for q in range(4):
+                engine.dma_start(
+                    out=plane[32 * q : 32 * q + 4].bitcast(I32),
+                    in_=rows[:, 4 * q : 4 * q + 4, :].rearrange("a r n -> r a n").bitcast(I32),
+                )
+
+        def load_weight_half(w, a):
+            raw = sbuf([P, PACK, HALF], F32, "stage", 2)
+            nc.sync.dma_start(out=raw[:], in_=w[:, a * HALF : (a + 1) * HALF].rearrange("(p j) c -> p j c", j=PACK))
+            return raw
+
+        def quantize_dealt(engine, raw, codes, scales):
+            grouped = sbuf([P, PACK * HALF], BF16, "grouped", 2)
+            dst = grouped[:].rearrange("p (t m j) -> p m t j", t=PACK, j=PACK)
+            src = raw.rearrange("p j (m t) -> p m t j", t=PACK)
+            if engine == "V":
+                nc.vector.tensor_copy(out=dst, in_=src)
+            elif engine == "G":
+                nc.gpsimd.tensor_scalar(dst, src, 1.0, 0.0, MULT, ADD)
+            else:
+                nc.scalar.copy(out=dst, in_=src)
+            nc.vector.quantize_mx(out=codes.bitcast(FP8X4), scales=scales, in_=grouped[:])
+
+        tab_plane = sbuf([P, 1, T], U8, "tab_plane")
+        nc.vector.memset(tab_plane[:].bitcast(I32), 0)
+        w2_plane_raw = sbuf([P, 1, H], U8, "w2_plane_raw")
+        nc.vector.memset(w2_plane_raw[:].bitcast(I32), 0)
+        w5_plane_raw = sbuf([P, 2, H], U8, "w5_plane_raw")
+        nc.vector.memset(w5_plane_raw[:].bitcast(I32), 0)
+        zero_in = sbuf([P, 1], F32, "zero_in")
+        nc.vector.memset(zero_in[:], 0.0)
+        zero = sbuf([P, 1], F32, "zero")
+        nc.scalar.activation(zero[:], zero_in[:], ACT.Silu)
+        ident = sbuf([P, P], F32, "ident")
+        make_identity(nc, ident[:])
+
+        idx = load_list(offs, "idx")
+        w2_raw = sbuf([P, 2 * H], U8, "w2_raw")
+        nc.sync.dma_start(out=w2_raw[:].bitcast(I32), in_=w2_words[0].bitcast(I32))
+        w3_raw = [load_weight_half(w3, 0)]
+        load_scale_rows(nc.sync, tab_plane, tab_scales)
+        tab = sbuf([P, T], U32, "tab")
+        nc.sync.dma_start(out=tab[:].bitcast(I32), in_=tab_words[0].rearrange("p n t -> p (n t)").bitcast(I32))
+        load_scale_rows(nc.sync, w2_plane_raw, w2_scales)
+        w1_raw = [load_weight_half(w1, 0)]
+        w5_raw = sbuf([P, 2, 2 * H], U8, "xs")
+        nc.sync.dma_start(out=w5_raw[:].bitcast(I32), in_=w5_words.rearrange("a p n -> p a n").bitcast(I32))
+        load_scale_rows(nc.sync, w5_plane_raw, w5_scales)
+        idx2 = load_list(offs2, "idx2")
+        page_rows = page0.rearrange("(a p t) c -> a t p c", a=2, t=PACK)
+        pages = []
+
+        def load_page(i):
+            page = sbuf([P, T2], F32, "page%d" % i)
+            nc.sync.dma_start(out=page[:], in_=page_rows[i // PACK, i % PACK])
+            pages.append(page)
+
+        def load_wgs(pair):
+            tile = sbuf([P, 2, S], F32, "wgs%d" % pair)
+            rows = wgs.rearrange("(p t) j -> p t j", t=PACK)[:, 2 * pair : 2 * pair + 2, :]
+            for q in range(4):
+                nc.sync.dma_start(out=tile[32 * q : 32 * q + 32], in_=rows)
+            return tile
+
+        wgs_dealt = [load_wgs(0)]
+        load_page(0)
+        load_page(1)
+        idx3 = load_list(offs3, "idx3")
+        wgs_dealt.append(load_wgs(1))
+        load_page(2)
+        load_page(3)
+        idx4 = load_list(offs4, "idx4")
+        gs_col = sbuf([P, 2, PACK], F32, "gs_col")
+        nc.sync.dma_start(out=gs_col[:], in_=gs.rearrange("(a p t) -> p a t", a=2, t=PACK))
+
+        def deal(codes, raw, plane, plane_raw):
+            for b in range(2):
+                nc.vector.tensor_copy(
+                    out=codes[:, b * H : (b + 1) * H].rearrange("p (t m e) -> p t m e", t=PACK, e=2),
+                    in_=raw[:, b * H : (b + 1) * H].rearrange("p (m t e) -> p t m e", t=PACK, e=2),
+                )
+            nc.vector.tensor_copy(
+                out=plane.rearrange("p (b t m) -> p b t m", b=2, t=PACK),
+                in_=plane_raw.rearrange("p (b m t) -> p b t m", b=2, t=PACK),
+            )
+
+        w1_codes = [sbuf([P, HALF], U32, "w1_codes%d" % a) for a in range(2)]
+        w1_plane = [sbuf([P, HALF], U8, "w1_plane%d" % a) for a in range(2)]
+        w3_codes = [sbuf([P, HALF], U32, "w3_codes%d" % a) for a in range(2)]
+        w3_plane = [sbuf([P, HALF], U8, "w3_plane%d" % a) for a in range(2)]
+        quantize_dealt("V", w3_raw[0][:], w3_codes[0][:], w3_plane[0][:])
+        w2_codes = sbuf([P, 2 * H], U8, "w2_codes")
+        w2_plane = sbuf([P, H], U8, "w2_plane")
+        deal(w2_codes[:], w2_raw[:], w2_plane[:], w2_plane_raw[:, 0, :])
+        v_codes, v_plane = [], []
+
+        def gather_table(jh):
+            entries = idx[:, jh * 32 : (jh + 1) * 32]
+            codes = sbuf([P, HALF], U32, "v_codes%d" % jh)
+            nc.vector.tensor_copy(codes[:], tab[:].indirect(entries))
+            plane = sbuf([P, HALF], U8, "v_plane%d" % jh)
+            nc.vector.tensor_copy(plane[:], tab_plane[:, 0, :].indirect(entries))
+            v_codes.append(codes)
+            v_plane.append(plane)
+
+        gather_table(0)
+        quantize_dealt("V", w1_raw[0][:], w1_codes[0][:], w1_plane[0][:])
+        gather_table(1)
+
+        w5_codes = sbuf([P, 2, 2 * H], U8, "w5_codes")
+        w5_plane = sbuf([P, 2, H], U8, "w5_plane")
+        for a in range(2):
+            deal(w5_codes[:, a, :], w5_raw[:, a, :], w5_plane[:, a, :], w5_plane_raw[:, a, :])
+
+        def transpose_sum(dst, first, second):
+            for jb in range(4):
+                cols = slice(jb * P, (jb + 1) * P)
+                nc.tensor.matmul(dst[:, cols], first[jb], ident[:], start=True, stop=False, is_transpose=True)
+                nc.tensor.matmul(dst[:, cols], second[jb], ident[:], start=False, stop=True, is_transpose=True)
+
+        def blocks(tile):
+            return [tile[:, jb * P : (jb + 1) * P] for jb in range(4)]
+
+        def sine(n, a, jh, t):
+            cols = slice(t * P, (t + 1) * P)
+            d = bank("d")
+            nc.tensor.matmul_mx(
+                d[:], lhsT=w3_codes[a][:, cols].bitcast(FP8X4), lhsT_scale=w3_plane[a][:, cols],
+                rhs=v_codes[jh][:].bitcast(FP8X4), rhs_scale=v_plane[jh][:], start=True, stop=True,
+            )
+            turns = sbuf([P, HALF], F32, "turns", 2)
+            nc.scalar.activation(turns[:], d[:], ACT.Copy, scale=1.0 / (2.0 * math.pi))
+            whole = sbuf([P, HALF], U32, "whole", 2)
+            if n < 2:
+                nc.scalar.activation(whole[:], turns[:], ACT.Copy, bias=ROUNDER)
+            else:
+                nc.gpsimd.tensor_scalar(whole[:].bitcast(I32), turns[:], 1.0, ROUNDER, MULT, ADD)
+            minus_whole = sbuf([P, HALF], F32, "minus_whole", 2)
+            nc.scalar.activation(minus_whole[:], whole[:], ACT.Copy, scale=-1.0, bias=ROUNDER)
+            part = bank("part")
+            transpose_sum(part, blocks(turns), blocks(minus_whole))
+            sin_d = sbuf([P, HALF], F32, "sin_d", 2)
+            nc.scalar.activation(sin_d[:], part[:], ACT.Sin, bias=zero[:], scale=2.0 * math.pi)
+            return sin_d
+
+        def tanh_and_f(a, jh, t):
+            b, f = bank("bf"), bank("bf")
+            cols = slice(t * P, (t + 1) * P)
+            for jb in range(4):
+                js = slice(jb * P, (jb + 1) * P)
+                nc.tensor.matmul_mx(
+                    b[:, js], lhsT=v_codes[jh][:, js].bitcast(FP8X4), lhsT_scale=v_plane[jh][:, js],
+                    rhs=w2_codes[:, a * H + 2 * t * P : a * H + 2 * (t + 1) * P].bitcast(FP4X4),
+                    rhs_scale=w2_plane[:, a * HALF + t * P : a * HALF + (t + 1) * P],
+                    start=True, stop=True,
+                )
+            tanh_b = sbuf([P, HALF], F32, "tanh_b", 3)
+            nc.scalar.activation(tanh_b[:], b[:], ACT.Tanh, bias=zero[:])
+            for jb in range(4):
+                js = slice(jb * P, (jb + 1) * P)
+                nc.tensor.matmul_mx(
+                    f[:, js], lhsT=v_codes[jh][:, js].bitcast(FP8X4), lhsT_scale=v_plane[jh][:, js],
+                    rhs=w1_codes[a][:, cols].bitcast(FP8X4), rhs_scale=w1_plane[a][:, cols], start=True, stop=True,
+                )
+            f_sb = sbuf([P, HALF], F32, "f_sb", 3)
+            nc.scalar.copy(f_sb[:], f[:])
+            return tanh_b, f_sb
+
+        def place(n, a, jh, t, sin_d, tanh_b, f_sb):
+            prod = sbuf([P, HALF], F32, "prod", 2)
+            engine = nc.vector if n < 1 else nc.gpsimd
+            engine.tensor_tensor(prod[:], tanh_b[:], sin_d[:], MULT)
+            h = bank("h")
+            transpose_sum(h, blocks(prod), blocks(f_sb))
+            h_sb = sbuf([P, HALF], F32, "h_sb", 2)
+            nc.scalar.copy(h_sb[:], h[:])
+            window = pages[a * PACK + t][:].indirect(idx2[:, jh * 32 : (jh + 1) * 32])
+            weights = wgs_dealt[t // 2][:, t % 2, jh * HALF : (jh + 1) * HALF]
+            if n < 1:
+                nc.vector.tensor_tensor(window, h_sb[:], weights, MULT)
+            else:
+                new = sbuf([P, HALF], F32, "new", 3)
+                nc.gpsimd.tensor_tensor(new[:], h_sb[:], weights, MULT)
+                nc.vector.tensor_copy(window, new[:])
+            return h_sb
+
+        w4_codes = [sbuf([P, H], U32, "w4_codes%d" % a) for a in range(2)]
+        w4_plane = [sbuf([P, H], U8, "w4_plane%d" % a) for a in range(2)]
+
+        def quantize_w4(a):
+            raw = sbuf([P, PACK, H], F32, "tab")
+            nc.sync.dma_start(out=raw[:], in_=w4[a * HALF : (a + 1) * HALF, :].rearrange("(p j) n -> p j n", j=PACK))
+            for b in range(2):
+                cols = slice(b * HALF, (b + 1) * HALF)
+                quantize_dealt("GSGS"[2 * a + b], raw[:, :, cols], w4_codes[a][:, cols], w4_plane[a][:, cols])
+
+        x_codes, x_plane = [], []
+
+        def fetch_x(a, t, xs):
+            nc.vector.tensor_copy(xs[:, t, :], pages[a * PACK + t][:].indirect(idx3[:]))
+
+        def quantize_x(a, xs, late):
+            nc.scalar.copy(late[:, 0:PACK], gs_col[:, a, :])
+            for t in range(PACK):
+                nc.scalar.activation(xs[:, t, :], xs[:, t, :], ACT.Copy, scale=late[:, t : t + 1])
+            codes = sbuf([P, 2, M], U32, "tab_plane" if a == 0 else "x_codes1")
+            plane = sbuf([P, 2, M], U8, "x_plane%d" % a)
+            src = xs[:].rearrange("p t (c i) -> p c t i", i=4)
+            for s, func in enumerate((ACT.Copy, ACT.Square)):
+                grouped = sbuf([P, PACK * M], BF16, "grouped", 2)
+                dst = grouped[:].rearrange("p (c i t) -> p c t i", i=4, t=PACK)
+                if s == 0 and "SG"[a] == "G":
+                    nc.gpsimd.tensor_scalar(dst, src, 1.0, 0.0, MULT, ADD)
+                elif s == 0 and "SG"[a] == "V":
+                    nc.vector.tensor_copy(out=dst, in_=src)
+                else:
+                    nc.scalar.activation(dst, src, func)
+                nc.vector.quantize_mx(out=codes[:, s, :].bitcast(FP8X4), scales=plane[:, s, :], in_=grouped[:])
+            x_codes.append(codes)
+            x_plane.append(plane)
+
+        units = [(a, jh, 2 * pair + e) for a in range(2) for pair in range(2) for jh in range(2) for e in range(2)]
+        fronts = {}
+        xs = [None, None]
+        for n in range(len(units) + 1):
+            if n == 3:
+                w3_raw.append(load_weight_half(w3, 1))
+                w1_raw.append(load_weight_half(w1, 1))
+                quantize_dealt("V", w3_raw[1][:], w3_codes[1][:], w3_plane[1][:])
+                quantize_dealt("V", w1_raw[1][:], w1_codes[1][:], w1_plane[1][:])
+                for i in range(4, 8):
+                    load_page(i)
+            if n == 7:
+                quantize_w4(0)
+            if n == 11:
+                quantize_w4(1)
+            if n < len(units):
+                fronts[n] = (sine(n, *units[n]),) + tanh_and_f(*units[n])
+            m = n - 1
+            if m >= 0:
+                a, jh, t = units[m]
+                place(m, a, jh, t, *fronts[m])
+                if jh == 1:
+                    if t == 0:
+                        xs[a] = sbuf([P, PACK, M], F32, "xs")
+                    fetch_x(a, t, xs[a])
+                if m == 10 or m == 15:
+                    quantize_x(m // 15, xs[m // 15], fronts[m][2])
+
+        inlet = [sbuf([P, PACK, M], F32, "wgs%d" % b) for b in range(2)]
+        out_rows = out.rearrange("(a p t) m -> a t p m", a=2, t=PACK)
+        ys = [bank(tag) for tag in ("bf", "bf", "d", "d", "part", "part", "h", "h")]
+        for a in range(2):
+            for i in range(8):
+                for s in range(2):
+                    cols = slice(i * P, (i + 1) * P)
+                    if s == 0:
+                        lhs, lhs_scale = w4_codes[a][:, cols].bitcast(FP8X4), w4_plane[a][:, cols]
+                    else:
+                        lhs, lhs_scale = w5_codes[:, a, 2 * i * P : 2 * (i + 1) * P].bitcast(FP4X4), w5_plane[:, a, cols]
+                    nc.tensor.matmul_mx(
+                        ys[i][:], lhsT=lhs, lhsT_scale=lhs_scale,
+                        rhs=x_codes[a][:, s, :].bitcast(FP8X4), rhs_scale=x_plane[a][:, s, :],
+                        start=(a == 0 and s == 0), stop=(a == 1 and s == 1),
+                    )
+        for i in range(8):
+            nc.vector.tensor_copy(inlet[i // PACK][:, i % PACK, :], pages[i][:].indirect(idx4[:]))
+        for i in range(8):
+            b, t = i // PACK, i % PACK
+            nc.vector.scalar_tensor_tensor(
+                inlet[b][:, t, :], ys[i][:], gs_col[:, b, t : t + 1], inlet[b][:, t, :], MULT, MULT
+            )
+            nc.sync.dma_start(out=out_rows[b, t], in_=inlet[b][:, t, :])

@@ -53,8 +53,8 @@ def tile_list_digester_layer_features_kernel(
                     in_=rows[:, 4 * q : 4 * q + 4, :].rearrange("a r n -> r a n").bitcast(I32),
                 )
 
-        def load_weight_half(w, a):
-            raw = sbuf([P, PACK, HALF], F32, "stage", 2)
+        def load_weight_half(w, a, tag):
+            raw = sbuf([P, PACK, HALF], F32, tag)
             nc.sync.dma_start(out=raw[:], in_=w[:, a * HALF : (a + 1) * HALF].rearrange("(p j) c -> p j c", j=PACK))
             return raw
 
@@ -86,15 +86,12 @@ def tile_list_digester_layer_features_kernel(
         idx = load_list(offs, "idx")
         w2_raw = sbuf([P, 2 * H], U8, "w2_raw")
         nc.sync.dma_start(out=w2_raw[:].bitcast(I32), in_=w2_words[0].bitcast(I32))
-        w3_raw = [load_weight_half(w3, 0)]
+        w3_raw = [load_weight_half(w3, 0, "wgs0")]
         load_scale_rows(nc.sync, tab_plane, tab_scales)
         tab = sbuf([P, T], U32, "tab")
         nc.sync.dma_start(out=tab[:].bitcast(I32), in_=tab_words[0].rearrange("p n t -> p (n t)").bitcast(I32))
         load_scale_rows(nc.sync, w2_plane_raw, w2_scales)
-        w1_raw = [load_weight_half(w1, 0)]
-        w5_raw = sbuf([P, 2, 2 * H], U8, "xs")
-        nc.sync.dma_start(out=w5_raw[:].bitcast(I32), in_=w5_words.rearrange("a p n -> p a n").bitcast(I32))
-        load_scale_rows(nc.sync, w5_plane_raw, w5_scales)
+        w1_raw = [load_weight_half(w1, 0, "stage1")]
         idx2 = load_list(offs2, "idx2")
         page_rows = page0.rearrange("(a p t) c -> a t p c", a=2, t=PACK)
         pages = []
@@ -104,23 +101,12 @@ def tile_list_digester_layer_features_kernel(
             nc.sync.dma_start(out=page[:], in_=page_rows[i // PACK, i % PACK])
             pages.append(page)
 
-        def load_wgs(pair):
+        def load_wgs(pair, queues):
             tile = sbuf([P, 2, S], F32, "wgs%d" % pair)
             rows = wgs.rearrange("(p t) j -> p t j", t=PACK)[:, 2 * pair : 2 * pair + 2, :]
             for q in range(4):
-                nc.sync.dma_start(out=tile[32 * q : 32 * q + 32], in_=rows)
+                queues[q].dma_start(out=tile[32 * q : 32 * q + 32], in_=rows)
             return tile
-
-        wgs_dealt = [load_wgs(0)]
-        load_page(0)
-        load_page(1)
-        idx3 = load_list(offs3, "idx3")
-        wgs_dealt.append(load_wgs(1))
-        load_page(2)
-        load_page(3)
-        idx4 = load_list(offs4, "idx4")
-        gs_col = sbuf([P, 2, PACK], F32, "gs_col")
-        nc.sync.dma_start(out=gs_col[:], in_=gs.rearrange("(a p t) -> p a t", a=2, t=PACK))
 
         def deal(codes, raw, plane, plane_raw):
             for b in range(2):
@@ -155,11 +141,22 @@ def tile_list_digester_layer_features_kernel(
         gather_table(0)
         quantize_dealt("V", w1_raw[0][:], w1_codes[0][:], w1_plane[0][:])
         gather_table(1)
-
-        w5_codes = sbuf([P, 2, 2 * H], U8, "w5_codes")
-        w5_plane = sbuf([P, 2, H], U8, "w5_plane")
-        for a in range(2):
-            deal(w5_codes[:, a, :], w5_raw[:, a, :], w5_plane[:, a, :], w5_plane_raw[:, a, :])
+        wgs_dealt = [load_wgs(0, [nc.gpsimd] * 4)]
+        load_page(0)
+        load_page(1)
+        idx3 = load_list(offs3, "idx3")
+        w3_raw.append(load_weight_half(w3, 1, "stage0"))
+        w1_raw.append(load_weight_half(w1, 1, "stage1"))
+        wgs_dealt.append(load_wgs(1, [nc.sync] * 4))
+        load_page(2)
+        load_page(3)
+        gs_col = sbuf([P, 2, PACK], F32, "gs_col")
+        nc.sync.dma_start(out=gs_col[:], in_=gs.rearrange("(a p t) -> p a t", a=2, t=PACK))
+        idx4 = load_list(offs4, "idx4")
+        load_page(4)
+        load_page(5)
+        load_page(6)
+        load_page(7)
 
         def transpose_sum(dst, first, second):
             for jb in range(4):
@@ -273,16 +270,21 @@ def tile_list_digester_layer_features_kernel(
         xs = [None, None]
         for n in range(len(units) + 1):
             if n == 3:
-                w3_raw.append(load_weight_half(w3, 1))
-                w1_raw.append(load_weight_half(w1, 1))
                 quantize_dealt("V", w3_raw[1][:], w3_codes[1][:], w3_plane[1][:])
                 quantize_dealt("V", w1_raw[1][:], w1_codes[1][:], w1_plane[1][:])
-                for i in range(4, 8):
-                    load_page(i)
             if n == 7:
                 quantize_w4(0)
             if n == 11:
                 quantize_w4(1)
+            if n == 6:
+                w5_raw = sbuf([P, 2, 2 * H], U8, "w5_raw")
+                nc.sync.dma_start(out=w5_raw[:].bitcast(I32), in_=w5_words.rearrange("a p n -> p a n").bitcast(I32))
+                load_scale_rows(nc.sync, w5_plane_raw, w5_scales)
+                w5_codes = sbuf([P, 2, 2 * H], U8, "w5_codes")
+                w5_plane = sbuf([P, 2, H], U8, "w5_plane")
+                for a in range(2):
+                    deal(w5_codes[:, a, :], w5_raw[:, a, :], w5_plane[:, a, :], w5_plane_raw[:, a, :])
+
             if n < len(units):
                 fronts[n] = (sine(n, *units[n]),) + tanh_and_f(*units[n])
             m = n - 1

@@ -39,7 +39,7 @@ def tile_list_digester_layer_features_kernel(
             return sb.tile(shape, dtype, name=tag, tag=tag, bufs=bufs, align_bytes=64)
 
         def bank(tag):
-            return psum.tile([P, HALF], F32, name=tag, tag=tag)
+            return psum.tile([P, HALF], F32, name=tag, tag=tag, bufs=4 if tag == "part" else 2)
 
         def load_list(src, name):
             tile = lists.tile([P, src.shape[1]], U16, name=name)
@@ -59,7 +59,7 @@ def tile_list_digester_layer_features_kernel(
             return raw
 
         def quantize_dealt(engine, raw, codes, scales):
-            grouped = sbuf([P, PACK * HALF], BF16, "grouped", 2)
+            grouped = sbuf([P, PACK * HALF], BF16, "grouped", 5)
             dst = grouped[:].rearrange("p (t m j) -> p m t j", t=PACK, j=PACK)
             src = raw.rearrange("p j (m t) -> p m t j", t=PACK)
             if engine == "V":
@@ -92,6 +92,9 @@ def tile_list_digester_layer_features_kernel(
         nc.sync.dma_start(out=tab[:].bitcast(I32), in_=tab_words[0].rearrange("p n t -> p (n t)").bitcast(I32))
         load_scale_rows(nc.sync, w2_plane_raw, w2_scales)
         w1_raw = [load_weight_half(w1, 0, "stage1")]
+        w5_raw = sbuf([P, 2, 2 * H], U8, "xs1")
+        nc.sync.dma_start(out=w5_raw[:].bitcast(I32), in_=w5_words.rearrange("a p n -> p a n").bitcast(I32))
+        load_scale_rows(nc.sync, w5_plane_raw, w5_scales)
         idx2 = load_list(offs2, "idx2")
         page_rows = page0.rearrange("(a p t) c -> a t p c", a=2, t=PACK)
         pages = []
@@ -109,11 +112,10 @@ def tile_list_digester_layer_features_kernel(
             return tile
 
         def deal(codes, raw, plane, plane_raw):
-            for b in range(2):
-                nc.vector.tensor_copy(
-                    out=codes[:, b * H : (b + 1) * H].rearrange("p (t m e) -> p t m e", t=PACK, e=2),
-                    in_=raw[:, b * H : (b + 1) * H].rearrange("p (m t e) -> p t m e", t=PACK, e=2),
-                )
+            nc.vector.tensor_copy(
+                out=codes.bitcast(U16).rearrange("p (b t m) -> p b t m", b=2, t=PACK),
+                in_=raw.bitcast(U16).rearrange("p (b m t) -> p b t m", b=2, t=PACK),
+            )
             nc.vector.tensor_copy(
                 out=plane.rearrange("p (b t m) -> p b t m", b=2, t=PACK),
                 in_=plane_raw.rearrange("p (b m t) -> p b t m", b=2, t=PACK),
@@ -142,11 +144,11 @@ def tile_list_digester_layer_features_kernel(
         quantize_dealt("V", w1_raw[0][:], w1_codes[0][:], w1_plane[0][:])
         gather_table(1)
         wgs_dealt = [load_wgs(0, [nc.gpsimd] * 4)]
-        load_page(0)
-        load_page(1)
-        idx3 = load_list(offs3, "idx3")
         w3_raw.append(load_weight_half(w3, 1, "stage0"))
+        load_page(0)
         w1_raw.append(load_weight_half(w1, 1, "stage1"))
+        idx3 = load_list(offs3, "idx3")
+        load_page(1)
         wgs_dealt.append(load_wgs(1, [nc.sync] * 4))
         load_page(2)
         load_page(3)
@@ -157,6 +159,15 @@ def tile_list_digester_layer_features_kernel(
         load_page(5)
         load_page(6)
         load_page(7)
+        w4_rows = w4.rearrange("(a p j) n -> a p j n", a=2, j=PACK)
+        w4_first = sbuf([P, PACK, H], F32, "tab")
+        nc.sync.dma_start(out=w4_first[:], in_=w4_rows[0])
+        w4_raw = [w4_first[:, :, 0:HALF], w4_first[:, :, HALF:H]]
+
+        w5_codes = sbuf([P, 2, 2 * H], U8, "w5_codes")
+        w5_plane = sbuf([P, 2, H], U8, "w5_plane")
+        for a in range(2):
+            deal(w5_codes[:, a, :], w5_raw[:, a, :], w5_plane[:, a, :], w5_plane_raw[:, a, :])
 
         def transpose_sum(dst, first, second):
             for jb in range(4):
@@ -167,7 +178,7 @@ def tile_list_digester_layer_features_kernel(
         def blocks(tile):
             return [tile[:, jb * P : (jb + 1) * P] for jb in range(4)]
 
-        def sine(n, a, jh, t):
+        def reduce_angle(n, a, jh, t):
             cols = slice(t * P, (t + 1) * P)
             d = bank("d")
             nc.tensor.matmul_mx(
@@ -176,8 +187,8 @@ def tile_list_digester_layer_features_kernel(
             )
             turns = sbuf([P, HALF], F32, "turns", 2)
             nc.scalar.activation(turns[:], d[:], ACT.Copy, scale=1.0 / (2.0 * math.pi))
-            whole = sbuf([P, HALF], U32, "whole", 2)
-            if n < 2:
+            whole = sbuf([P, HALF], U32, "whole", 4)
+            if True:
                 nc.scalar.activation(whole[:], turns[:], ACT.Copy, bias=ROUNDER)
             else:
                 nc.gpsimd.tensor_scalar(whole[:].bitcast(I32), turns[:], 1.0, ROUNDER, MULT, ADD)
@@ -185,9 +196,10 @@ def tile_list_digester_layer_features_kernel(
             nc.scalar.activation(minus_whole[:], whole[:], ACT.Copy, scale=-1.0, bias=ROUNDER)
             part = bank("part")
             transpose_sum(part, blocks(turns), blocks(minus_whole))
-            sin_d = sbuf([P, HALF], F32, "sin_d", 2)
-            nc.scalar.activation(sin_d[:], part[:], ACT.Sin, bias=zero[:], scale=2.0 * math.pi)
-            return sin_d
+            return part, whole
+
+        def sine(part, sin_d):
+            nc.scalar.activation(sin_d, part[:], ACT.Sin, bias=zero[:], scale=2.0 * math.pi)
 
         def tanh_and_f(a, jh, t):
             b, f = bank("bf"), bank("bf")
@@ -200,7 +212,7 @@ def tile_list_digester_layer_features_kernel(
                     rhs_scale=w2_plane[:, a * HALF + t * P : a * HALF + (t + 1) * P],
                     start=True, stop=True,
                 )
-            tanh_b = sbuf([P, HALF], F32, "tanh_b", 3)
+            tanh_b = sbuf([P, HALF], F32, "tanh_b", 2)
             nc.scalar.activation(tanh_b[:], b[:], ACT.Tanh, bias=zero[:])
             for jb in range(4):
                 js = slice(jb * P, (jb + 1) * P)
@@ -208,21 +220,20 @@ def tile_list_digester_layer_features_kernel(
                     f[:, js], lhsT=v_codes[jh][:, js].bitcast(FP8X4), lhsT_scale=v_plane[jh][:, js],
                     rhs=w1_codes[a][:, cols].bitcast(FP8X4), rhs_scale=w1_plane[a][:, cols], start=True, stop=True,
                 )
-            f_sb = sbuf([P, HALF], F32, "f_sb", 3)
+            f_sb = sbuf([P, HALF], F32, "f_sb", 2)
             nc.scalar.copy(f_sb[:], f[:])
             return tanh_b, f_sb
 
-        def place(n, a, jh, t, sin_d, tanh_b, f_sb):
+        def place(n, a, jh, t, sin_d, tanh_b, f_sb, h):
             prod = sbuf([P, HALF], F32, "prod", 2)
-            engine = nc.vector if n < 1 else nc.gpsimd
-            engine.tensor_tensor(prod[:], tanh_b[:], sin_d[:], MULT)
-            h = bank("h")
+            engine = nc.vector if n < 16 else nc.gpsimd
+            engine.tensor_tensor(prod[:], tanh_b[:], sin_d, MULT)
             transpose_sum(h, blocks(prod), blocks(f_sb))
             h_sb = sbuf([P, HALF], F32, "h_sb", 2)
             nc.scalar.copy(h_sb[:], h[:])
             window = pages[a * PACK + t][:].indirect(idx2[:, jh * 32 : (jh + 1) * 32])
             weights = wgs_dealt[t // 2][:, t % 2, jh * HALF : (jh + 1) * HALF]
-            if n < 1:
+            if n < 16:
                 nc.vector.tensor_tensor(window, h_sb[:], weights, MULT)
             else:
                 new = sbuf([P, HALF], F32, "new", 3)
@@ -233,31 +244,27 @@ def tile_list_digester_layer_features_kernel(
         w4_codes = [sbuf([P, H], U32, "w4_codes%d" % a) for a in range(2)]
         w4_plane = [sbuf([P, H], U8, "w4_plane%d" % a) for a in range(2)]
 
-        def quantize_w4(a):
-            raw = sbuf([P, PACK, H], F32, "tab")
-            nc.sync.dma_start(out=raw[:], in_=w4[a * HALF : (a + 1) * HALF, :].rearrange("(p j) n -> p j n", j=PACK))
-            for b in range(2):
-                cols = slice(b * HALF, (b + 1) * HALF)
-                quantize_dealt("GSGS"[2 * a + b], raw[:, :, cols], w4_codes[a][:, cols], w4_plane[a][:, cols])
+        def quantize_w4(a, b):
+            cols = slice(b * HALF, (b + 1) * HALF)
+            quantize_dealt("SSSS"[2 * a + b], w4_raw[2 * a + b], w4_codes[a][:, cols], w4_plane[a][:, cols])
 
         x_codes, x_plane = [], []
 
         def fetch_x(a, t, xs):
             nc.vector.tensor_copy(xs[:, t, :], pages[a * PACK + t][:].indirect(idx3[:]))
 
-        def quantize_x(a, xs, late):
-            nc.scalar.copy(late[:, 0:PACK], gs_col[:, a, :])
+        def quantize_x(a, xs):
             for t in range(PACK):
-                nc.scalar.activation(xs[:, t, :], xs[:, t, :], ACT.Copy, scale=late[:, t : t + 1])
+                nc.scalar.activation(xs[:, t, :], xs[:, t, :], ACT.Copy, scale=gs_col[:, a, t : t + 1])
             codes = sbuf([P, 2, M], U32, "tab_plane" if a == 0 else "x_codes1")
             plane = sbuf([P, 2, M], U8, "x_plane%d" % a)
             src = xs[:].rearrange("p t (c i) -> p c t i", i=4)
             for s, func in enumerate((ACT.Copy, ACT.Square)):
-                grouped = sbuf([P, PACK * M], BF16, "grouped", 2)
+                grouped = sbuf([P, PACK * M], BF16, "grouped", 5)
                 dst = grouped[:].rearrange("p (c i t) -> p c t i", i=4, t=PACK)
-                if s == 0 and "SG"[a] == "G":
+                if s == 0 and "SS"[a] == "G":
                     nc.gpsimd.tensor_scalar(dst, src, 1.0, 0.0, MULT, ADD)
-                elif s == 0 and "SG"[a] == "V":
+                elif s == 0 and "SS"[a] == "V":
                     nc.vector.tensor_copy(out=dst, in_=src)
                 else:
                     nc.scalar.activation(dst, src, func)
@@ -265,42 +272,48 @@ def tile_list_digester_layer_features_kernel(
             x_codes.append(codes)
             x_plane.append(plane)
 
-        units = [(a, jh, 2 * pair + e) for a in range(2) for pair in range(2) for jh in range(2) for e in range(2)]
-        fronts = {}
+        units = [(a, jh, t) for a in range(2) for t in range(PACK) for jh in range(2)]
+        fronts, angles, sines = {}, {}, {}
         xs = [None, None]
-        for n in range(len(units) + 1):
+        for n in range(len(units) + 2):
             if n == 3:
                 quantize_dealt("V", w3_raw[1][:], w3_codes[1][:], w3_plane[1][:])
                 quantize_dealt("V", w1_raw[1][:], w1_codes[1][:], w1_plane[1][:])
-            if n == 7:
-                quantize_w4(0)
-            if n == 11:
-                quantize_w4(1)
-            if n == 6:
-                w5_raw = sbuf([P, 2, 2 * H], U8, "w5_raw")
-                nc.sync.dma_start(out=w5_raw[:].bitcast(I32), in_=w5_words.rearrange("a p n -> p a n").bitcast(I32))
-                load_scale_rows(nc.sync, w5_plane_raw, w5_scales)
-                w5_codes = sbuf([P, 2, 2 * H], U8, "w5_codes")
-                w5_plane = sbuf([P, 2, H], U8, "w5_plane")
-                for a in range(2):
-                    deal(w5_codes[:, a, :], w5_raw[:, a, :], w5_plane[:, a, :], w5_plane_raw[:, a, :])
-
+            if n == 3:
+                for b in range(2):
+                    raw = sbuf([P, PACK, HALF], F32, "stage%d" % b)
+                    nc.sync.dma_start(out=raw[:], in_=w4_rows[1][:, :, b * HALF : (b + 1) * HALF])
+                    w4_raw.append(raw[:])
             if n < len(units):
-                fronts[n] = (sine(n, *units[n]),) + tanh_and_f(*units[n])
-            m = n - 1
-            if m >= 0:
+                angles[n] = reduce_angle(n, *units[n])
+            if n < 2:
+                sines[n] = sbuf([P, HALF], F32, "sin_d", 2)[:]
+                sine(angles[n][0], sines[n])
+            k = n - 1
+            if 2 <= k < len(units):
+                sines[k] = angles[n][1][:].bitcast(F32) if n < len(units) else sbuf([P, HALF], F32, "sin_d", 2)[:]
+                sine(angles[k][0], sines[k])
+            if n < len(units):
+                fronts[n] = tanh_and_f(*units[n])
+            for m in ([n] if n < 2 else []) + ([n - 2] if n - 2 >= 2 else []):
                 a, jh, t = units[m]
-                place(m, a, jh, t, *fronts[m])
+                h = angles[m + 1][0] if 2 <= m < len(units) - 1 else angles[m][0]
+                place(m, a, jh, t, sines[m], *fronts[m], h)
                 if jh == 1:
                     if t == 0:
-                        xs[a] = sbuf([P, PACK, M], F32, "xs")
+                        xs[a] = sbuf([P, PACK, M], F32, "xs%d" % a)
                     fetch_x(a, t, xs[a])
-                if m == 10 or m == 15:
-                    quantize_x(m // 15, xs[m // 15], fronts[m][2])
 
-        inlet = [sbuf([P, PACK, M], F32, "wgs%d" % b) for b in range(2)]
+        quantize_x(0, xs[0])
+        quantize_w4(0, 0)
+        quantize_w4(0, 1)
+        quantize_w4(1, 0)
+        quantize_w4(1, 1)
+        quantize_x(1, xs[1])
+
+        inlet = [sbuf([P, PACK, M], F32, tag) for tag in ("stage1", "xs1")]
         out_rows = out.rearrange("(a p t) m -> a t p m", a=2, t=PACK)
-        ys = [bank(tag) for tag in ("bf", "bf", "d", "d", "part", "part", "h", "h")]
+        ys = [bank(tag) for tag in ("bf", "bf", "d", "d", "part", "part", "part", "part")]
         for a in range(2):
             for i in range(8):
                 for s in range(2):

@@ -39,7 +39,7 @@ def tile_list_digester_layer_features_kernel(
             return sb.tile(shape, dtype, name=tag, tag=tag, bufs=bufs, align_bytes=64)
 
         def bank(tag):
-            return psum.tile([P, HALF], F32, name=tag, tag=tag, bufs=4 if tag == "part" else 2)
+            return psum.tile([P, HALF], F32, name=tag, tag=tag, bufs=2)
 
         def load_list(src, name):
             tile = lists.tile([P, src.shape[1]], U16, name=name)
@@ -59,7 +59,7 @@ def tile_list_digester_layer_features_kernel(
             return raw
 
         def quantize_dealt(engine, raw, codes, scales):
-            grouped = sbuf([P, PACK * HALF], BF16, "grouped", 5)
+            grouped = sbuf([P, PACK * HALF], BF16, "grouped", 4)
             dst = grouped[:].rearrange("p (t m j) -> p m t j", t=PACK, j=PACK)
             src = raw.rearrange("p j (m t) -> p m t j", t=PACK)
             if engine == "V":
@@ -156,13 +156,13 @@ def tile_list_digester_layer_features_kernel(
         nc.sync.dma_start(out=gs_col[:], in_=gs.rearrange("(a p t) -> p a t", a=2, t=PACK))
         idx4 = load_list(offs4, "idx4")
         load_page(4)
-        load_page(5)
-        load_page(6)
-        load_page(7)
         w4_rows = w4.rearrange("(a p j) n -> a p j n", a=2, j=PACK)
         w4_first = sbuf([P, PACK, H], F32, "tab")
         nc.sync.dma_start(out=w4_first[:], in_=w4_rows[0])
         w4_raw = [w4_first[:, :, 0:HALF], w4_first[:, :, HALF:H]]
+        load_page(5)
+        load_page(6)
+        load_page(7)
 
         w5_codes = sbuf([P, 2, 2 * H], U8, "w5_codes")
         w5_plane = sbuf([P, 2, H], U8, "w5_plane")
@@ -181,13 +181,15 @@ def tile_list_digester_layer_features_kernel(
         def reduce_angle(n, a, jh, t):
             cols = slice(t * P, (t + 1) * P)
             d = bank("d")
-            nc.tensor.matmul_mx(
-                d[:], lhsT=w3_codes[a][:, cols].bitcast(FP8X4), lhsT_scale=w3_plane[a][:, cols],
-                rhs=v_codes[jh][:].bitcast(FP8X4), rhs_scale=v_plane[jh][:], start=True, stop=True,
-            )
+            for jb in range(4):
+                js = slice(jb * P, (jb + 1) * P)
+                nc.tensor.matmul_mx(
+                    d[:, js], lhsT=v_codes[jh][:, js].bitcast(FP8X4), lhsT_scale=v_plane[jh][:, js],
+                    rhs=w3_codes[a][:, cols].bitcast(FP8X4), rhs_scale=w3_plane[a][:, cols], start=True, stop=True,
+                )
             turns = sbuf([P, HALF], F32, "turns", 2)
             nc.scalar.activation(turns[:], d[:], ACT.Copy, scale=1.0 / (2.0 * math.pi))
-            whole = sbuf([P, HALF], U32, "whole", 4)
+            whole = sbuf([P, HALF], U32, "whole", 2)
             if True:
                 nc.scalar.activation(whole[:], turns[:], ACT.Copy, bias=ROUNDER)
             else:
@@ -195,51 +197,44 @@ def tile_list_digester_layer_features_kernel(
             minus_whole = sbuf([P, HALF], F32, "minus_whole", 2)
             nc.scalar.activation(minus_whole[:], whole[:], ACT.Copy, scale=-1.0, bias=ROUNDER)
             part = bank("part")
-            transpose_sum(part, blocks(turns), blocks(minus_whole))
+            transpose_sum(part, blocks(minus_whole), blocks(turns))
             return part, whole
 
         def sine(part, sin_d):
             nc.scalar.activation(sin_d, part[:], ACT.Sin, bias=zero[:], scale=2.0 * math.pi)
 
-        def tanh_and_f(a, jh, t):
-            b, f = bank("bf"), bank("bf")
+        def tanh_and_f(n, a, jh, t):
+            b, f = bank("b"), bank("f")
             cols = slice(t * P, (t + 1) * P)
-            for jb in range(4):
-                js = slice(jb * P, (jb + 1) * P)
-                nc.tensor.matmul_mx(
-                    b[:, js], lhsT=v_codes[jh][:, js].bitcast(FP8X4), lhsT_scale=v_plane[jh][:, js],
-                    rhs=w2_codes[:, a * H + 2 * t * P : a * H + 2 * (t + 1) * P].bitcast(FP4X4),
-                    rhs_scale=w2_plane[:, a * HALF + t * P : a * HALF + (t + 1) * P],
-                    start=True, stop=True,
-                )
-            tanh_b = sbuf([P, HALF], F32, "tanh_b", 2)
+            nc.tensor.matmul_mx(
+                b[:], lhsT=w2_codes[:, a * H + 2 * t * P : a * H + 2 * (t + 1) * P].bitcast(FP4X4),
+                lhsT_scale=w2_plane[:, a * HALF + t * P : a * HALF + (t + 1) * P],
+                rhs=v_codes[jh][:].bitcast(FP8X4), rhs_scale=v_plane[jh][:], start=True, stop=True,
+            )
+            tanh_b = sbuf([P, HALF], F32, "tanh_b", 3)
             nc.scalar.activation(tanh_b[:], b[:], ACT.Tanh, bias=zero[:])
-            for jb in range(4):
-                js = slice(jb * P, (jb + 1) * P)
-                nc.tensor.matmul_mx(
-                    f[:, js], lhsT=v_codes[jh][:, js].bitcast(FP8X4), lhsT_scale=v_plane[jh][:, js],
-                    rhs=w1_codes[a][:, cols].bitcast(FP8X4), rhs_scale=w1_plane[a][:, cols], start=True, stop=True,
-                )
-            f_sb = sbuf([P, HALF], F32, "f_sb", 2)
+            nc.tensor.matmul_mx(
+                f[:], lhsT=w1_codes[a][:, cols].bitcast(FP8X4), lhsT_scale=w1_plane[a][:, cols],
+                rhs=v_codes[jh][:].bitcast(FP8X4), rhs_scale=v_plane[jh][:], start=True, stop=True,
+            )
+            if n < 0:
+                return tanh_b, f
+            f_sb = sbuf([P, HALF], F32, "f_sb", 3)
             nc.scalar.copy(f_sb[:], f[:])
             return tanh_b, f_sb
 
-        def place(n, a, jh, t, sin_d, tanh_b, f_sb, h):
+        def place(n, a, jh, t, sin_d, tanh_b, f):
             prod = sbuf([P, HALF], F32, "prod", 2)
-            engine = nc.vector if n < 16 else nc.gpsimd
-            engine.tensor_tensor(prod[:], tanh_b[:], sin_d, MULT)
-            transpose_sum(h, blocks(prod), blocks(f_sb))
-            h_sb = sbuf([P, HALF], F32, "h_sb", 2)
-            nc.scalar.copy(h_sb[:], h[:])
+            (nc.vector if n < 0 else nc.gpsimd).tensor_tensor(prod[:], tanh_b[:], sin_d[:], MULT)
+            (nc.vector if n < 0 else nc.gpsimd).tensor_tensor(prod[:], f[:], prod[:], ADD)
             window = pages[a * PACK + t][:].indirect(idx2[:, jh * 32 : (jh + 1) * 32])
             weights = wgs_dealt[t // 2][:, t % 2, jh * HALF : (jh + 1) * HALF]
-            if n < 16:
-                nc.vector.tensor_tensor(window, h_sb[:], weights, MULT)
+            if n < 0:
+                nc.vector.tensor_tensor(window, prod[:], weights, MULT)
             else:
                 new = sbuf([P, HALF], F32, "new", 3)
-                nc.gpsimd.tensor_tensor(new[:], h_sb[:], weights, MULT)
+                nc.gpsimd.tensor_tensor(new[:], prod[:], weights, MULT)
                 nc.vector.tensor_copy(window, new[:])
-            return h_sb
 
         w4_codes = [sbuf([P, H], U32, "w4_codes%d" % a) for a in range(2)]
         w4_plane = [sbuf([P, H], U8, "w4_plane%d" % a) for a in range(2)]
@@ -253,14 +248,15 @@ def tile_list_digester_layer_features_kernel(
         def fetch_x(a, t, xs):
             nc.vector.tensor_copy(xs[:, t, :], pages[a * PACK + t][:].indirect(idx3[:]))
 
-        def quantize_x(a, xs):
+        def quantize_x(a, xs, late):
+            nc.scalar.copy(late[:, 0:PACK], gs_col[:, a, :])
             for t in range(PACK):
-                nc.scalar.activation(xs[:, t, :], xs[:, t, :], ACT.Copy, scale=gs_col[:, a, t : t + 1])
+                nc.scalar.activation(xs[:, t, :], xs[:, t, :], ACT.Copy, scale=late[:, t : t + 1])
             codes = sbuf([P, 2, M], U32, "tab_plane" if a == 0 else "x_codes1")
             plane = sbuf([P, 2, M], U8, "x_plane%d" % a)
             src = xs[:].rearrange("p t (c i) -> p c t i", i=4)
             for s, func in enumerate((ACT.Copy, ACT.Square)):
-                grouped = sbuf([P, PACK * M], BF16, "grouped", 5)
+                grouped = sbuf([P, PACK * M], BF16, "grouped", 4)
                 dst = grouped[:].rearrange("p (c i t) -> p c t i", i=4, t=PACK)
                 if s == 0 and "SS"[a] == "G":
                     nc.gpsimd.tensor_scalar(dst, src, 1.0, 0.0, MULT, ADD)
@@ -275,45 +271,40 @@ def tile_list_digester_layer_features_kernel(
         units = [(a, jh, t) for a in range(2) for t in range(PACK) for jh in range(2)]
         fronts, angles, sines = {}, {}, {}
         xs = [None, None]
-        for n in range(len(units) + 2):
-            if n == 3:
+        for n in range(len(units) + 1):
+            if n == 5:
                 quantize_dealt("V", w3_raw[1][:], w3_codes[1][:], w3_plane[1][:])
-                quantize_dealt("V", w1_raw[1][:], w1_codes[1][:], w1_plane[1][:])
-            if n == 3:
+                quantize_dealt("S", w1_raw[1][:], w1_codes[1][:], w1_plane[1][:])
+            if n == 5:
                 for b in range(2):
                     raw = sbuf([P, PACK, HALF], F32, "stage%d" % b)
                     nc.sync.dma_start(out=raw[:], in_=w4_rows[1][:, :, b * HALF : (b + 1) * HALF])
                     w4_raw.append(raw[:])
             if n < len(units):
-                angles[n] = reduce_angle(n, *units[n])
-            if n < 2:
-                sines[n] = sbuf([P, HALF], F32, "sin_d", 2)[:]
-                sine(angles[n][0], sines[n])
-            k = n - 1
-            if 2 <= k < len(units):
-                sines[k] = angles[n][1][:].bitcast(F32) if n < len(units) else sbuf([P, HALF], F32, "sin_d", 2)[:]
-                sine(angles[k][0], sines[k])
-            if n < len(units):
-                fronts[n] = tanh_and_f(*units[n])
-            for m in ([n] if n < 2 else []) + ([n - 2] if n - 2 >= 2 else []):
+                part, whole = reduce_angle(n, *units[n])
+                fronts[n] = tanh_and_f(n, *units[n])
+                sines[n] = sbuf([P, HALF], F32, "sin_d", 3)
+                sine(part, sines[n][:])
+            m = n - 1
+            if m >= 0:
                 a, jh, t = units[m]
-                h = angles[m + 1][0] if 2 <= m < len(units) - 1 else angles[m][0]
-                place(m, a, jh, t, sines[m], *fronts[m], h)
+                place(m, a, jh, t, sines[m], *fronts[m])
                 if jh == 1:
                     if t == 0:
                         xs[a] = sbuf([P, PACK, M], F32, "xs%d" % a)
                     fetch_x(a, t, xs[a])
+                if m == 9:
+                    quantize_x(0, xs[0], sines[9])
 
-        quantize_x(0, xs[0])
         quantize_w4(0, 0)
         quantize_w4(0, 1)
         quantize_w4(1, 0)
         quantize_w4(1, 1)
-        quantize_x(1, xs[1])
+        quantize_x(1, xs[1], sines[15])
 
         inlet = [sbuf([P, PACK, M], F32, tag) for tag in ("stage1", "xs1")]
         out_rows = out.rearrange("(a p t) m -> a t p m", a=2, t=PACK)
-        ys = [bank(tag) for tag in ("bf", "bf", "d", "d", "part", "part", "part", "part")]
+        ys = [bank(tag) for tag in ("d", "d", "b", "b", "part", "part", "f", "f")]
         for a in range(2):
             for i in range(8):
                 for s in range(2):

@@ -22,7 +22,13 @@ ADD = mybir.AluOpType.add
 P = 128
 PACK = 4
 HALF = P * PACK
+LIST_COLS = HALF // 16
+TILES = H // P
 ROUNDER = 1.5 * 2.0**23
+UNITS_ON_VECTOR = 1
+SECOND_HALVES_AT = 5
+FIRST_X_AFTER = 10
+OUT_TILES_ON_GPSIMD = 3
 
 
 def tile_list_digester_layer_features_kernel(
@@ -39,38 +45,47 @@ def tile_list_digester_layer_features_kernel(
             return sb.tile(shape, dtype, name=tag, tag=tag, bufs=bufs, align_bytes=64)
 
         def bank(tag):
-            return psum.tile([P, HALF], F32, name=tag, tag=tag, bufs=2)
+            return psum.tile([P, HALF], F32, name=tag, tag=tag)
 
         def load_list(src, name):
             tile = lists.tile([P, src.shape[1]], U16, name=name)
             nc.sync.dma_start(tile[:], src)
             return tile
 
-        def load_scale_rows(engine, plane, rows):
+        def load_scale_rows(plane, rows):
             for q in range(4):
-                engine.dma_start(
+                nc.sync.dma_start(
                     out=plane[32 * q : 32 * q + 4].bitcast(I32),
                     in_=rows[:, 4 * q : 4 * q + 4, :].rearrange("a r n -> r a n").bitcast(I32),
                 )
 
-        def load_weight_half(w, a, tag):
+        def load_weight_columns(rows, b, tag):
             raw = sbuf([P, PACK, HALF], F32, tag)
-            nc.sync.dma_start(out=raw[:], in_=w[:, a * HALF : (a + 1) * HALF].rearrange("(p j) c -> p j c", j=PACK))
+            nc.sync.dma_start(out=raw[:], in_=rows[:, b * HALF : (b + 1) * HALF].rearrange("(p j) c -> p j c", j=PACK))
             return raw
 
-        def quantize_dealt(engine, raw, codes, scales):
-            grouped = sbuf([P, PACK * HALF], BF16, "grouped", 4)
-            dst = grouped[:].rearrange("p (t m j) -> p m t j", t=PACK, j=PACK)
-            src = raw.rearrange("p j (m t) -> p m t j", t=PACK)
-            if engine == "V":
-                nc.vector.tensor_copy(out=dst, in_=src)
-            elif engine == "G":
-                nc.gpsimd.tensor_scalar(dst, src, 1.0, 0.0, MULT, ADD)
-            else:
-                nc.scalar.copy(out=dst, in_=src)
-            nc.vector.quantize_mx(out=codes.bitcast(FP8X4), scales=scales, in_=grouped[:])
+        def grouped_tile():
+            return sbuf([P, PACK * HALF], BF16, "grouped", 4)
 
-        tab_plane = sbuf([P, 1, T], U8, "tab_plane")
+        def quantize_dealt(copy, raw, codes, plane):
+            grouped = grouped_tile()
+            copy(
+                out=grouped[:].rearrange("p (t m j) -> p m t j", t=PACK, j=PACK),
+                in_=raw.rearrange("p j (m t) -> p m t j", t=PACK),
+            )
+            nc.vector.quantize_mx(out=codes.bitcast(FP8X4), scales=plane, in_=grouped[:])
+
+        def deal_packed(codes, raw, plane, plane_raw):
+            nc.vector.tensor_copy(
+                out=codes.bitcast(U16).rearrange("p (b t m) -> p b t m", b=2, t=PACK),
+                in_=raw.bitcast(U16).rearrange("p (b m t) -> p b t m", b=2, t=PACK),
+            )
+            nc.vector.tensor_copy(
+                out=plane.rearrange("p (b t m) -> p b t m", b=2, t=PACK),
+                in_=plane_raw.rearrange("p (b m t) -> p b t m", b=2, t=PACK),
+            )
+
+        tab_plane = sbuf([P, 1, T], U8, "x_codes0")
         nc.vector.memset(tab_plane[:].bitcast(I32), 0)
         w2_plane_raw = sbuf([P, 1, H], U8, "w2_plane_raw")
         nc.vector.memset(w2_plane_raw[:].bitcast(I32), 0)
@@ -86,243 +101,209 @@ def tile_list_digester_layer_features_kernel(
         idx = load_list(offs, "idx")
         w2_raw = sbuf([P, 2 * H], U8, "w2_raw")
         nc.sync.dma_start(out=w2_raw[:].bitcast(I32), in_=w2_words[0].bitcast(I32))
-        w3_raw = [load_weight_half(w3, 0, "wgs0")]
-        load_scale_rows(nc.sync, tab_plane, tab_scales)
+        w3_raw = [load_weight_columns(w3, 0, "wgs0")]
+        load_scale_rows(tab_plane, tab_scales)
         tab = sbuf([P, T], U32, "tab")
         nc.sync.dma_start(out=tab[:].bitcast(I32), in_=tab_words[0].rearrange("p n t -> p (n t)").bitcast(I32))
-        load_scale_rows(nc.sync, w2_plane_raw, w2_scales)
-        w1_raw = [load_weight_half(w1, 0, "stage1")]
+        load_scale_rows(w2_plane_raw, w2_scales)
+        w1_raw = [load_weight_columns(w1, 0, "stage1")]
         w5_raw = sbuf([P, 2, 2 * H], U8, "xs1")
         nc.sync.dma_start(out=w5_raw[:].bitcast(I32), in_=w5_words.rearrange("a p n -> p a n").bitcast(I32))
-        load_scale_rows(nc.sync, w5_plane_raw, w5_scales)
+        load_scale_rows(w5_plane_raw, w5_scales)
         idx2 = load_list(offs2, "idx2")
-        page_rows = page0.rearrange("(a p t) c -> a t p c", a=2, t=PACK)
-        pages = []
-
-        def load_page(i):
-            page = sbuf([P, T2], F32, "page%d" % i)
-            nc.sync.dma_start(out=page[:], in_=page_rows[i // PACK, i % PACK])
-            pages.append(page)
-
-        def load_wgs(pair, queues):
-            tile = sbuf([P, 2, S], F32, "wgs%d" % pair)
-            rows = wgs.rearrange("(p t) j -> p t j", t=PACK)[:, 2 * pair : 2 * pair + 2, :]
-            for q in range(4):
-                queues[q].dma_start(out=tile[32 * q : 32 * q + 32], in_=rows)
-            return tile
-
-        def deal(codes, raw, plane, plane_raw):
-            nc.vector.tensor_copy(
-                out=codes.bitcast(U16).rearrange("p (b t m) -> p b t m", b=2, t=PACK),
-                in_=raw.bitcast(U16).rearrange("p (b m t) -> p b t m", b=2, t=PACK),
-            )
-            nc.vector.tensor_copy(
-                out=plane.rearrange("p (b t m) -> p b t m", b=2, t=PACK),
-                in_=plane_raw.rearrange("p (b m t) -> p b t m", b=2, t=PACK),
-            )
 
         w1_codes = [sbuf([P, HALF], U32, "w1_codes%d" % a) for a in range(2)]
         w1_plane = [sbuf([P, HALF], U8, "w1_plane%d" % a) for a in range(2)]
         w3_codes = [sbuf([P, HALF], U32, "w3_codes%d" % a) for a in range(2)]
         w3_plane = [sbuf([P, HALF], U8, "w3_plane%d" % a) for a in range(2)]
-        quantize_dealt("V", w3_raw[0][:], w3_codes[0][:], w3_plane[0][:])
         w2_codes = sbuf([P, 2 * H], U8, "w2_codes")
         w2_plane = sbuf([P, H], U8, "w2_plane")
-        deal(w2_codes[:], w2_raw[:], w2_plane[:], w2_plane_raw[:, 0, :])
         v_codes, v_plane = [], []
 
-        def gather_table(jh):
-            entries = idx[:, jh * 32 : (jh + 1) * 32]
-            codes = sbuf([P, HALF], U32, "v_codes%d" % jh)
+        def gather_table(half):
+            entries = idx[:, half * LIST_COLS : (half + 1) * LIST_COLS]
+            codes = sbuf([P, HALF], U32, "v_codes%d" % half)
             nc.vector.tensor_copy(codes[:], tab[:].indirect(entries))
-            plane = sbuf([P, HALF], U8, "v_plane%d" % jh)
+            plane = sbuf([P, HALF], U8, "v_plane%d" % half)
             nc.vector.tensor_copy(plane[:], tab_plane[:, 0, :].indirect(entries))
             v_codes.append(codes)
             v_plane.append(plane)
 
+        quantize_dealt(nc.vector.tensor_copy, w3_raw[0][:], w3_codes[0][:], w3_plane[0][:])
+        deal_packed(w2_codes[:], w2_raw[:], w2_plane[:], w2_plane_raw[:, 0, :])
         gather_table(0)
-        quantize_dealt("V", w1_raw[0][:], w1_codes[0][:], w1_plane[0][:])
+        quantize_dealt(nc.vector.tensor_copy, w1_raw[0][:], w1_codes[0][:], w1_plane[0][:])
         gather_table(1)
-        wgs_dealt = [load_wgs(0, [nc.gpsimd] * 4)]
-        w3_raw.append(load_weight_half(w3, 1, "stage0"))
-        load_page(0)
-        w1_raw.append(load_weight_half(w1, 1, "stage1"))
+
+        def load_wgs(pair, queue):
+            wgs_tile = sbuf([P, 2, S], F32, "wgs%d" % pair)
+            wgs_rows = wgs.rearrange("(p t) j -> p t j", t=PACK)[:, 2 * pair : 2 * pair + 2, :]
+            for q in range(4):
+                queue.dma_start(out=wgs_tile[32 * q : 32 * q + 32], in_=wgs_rows)
+            return wgs_tile
+
+        page_rows = page0.rearrange("(a p t) c -> a t p c", a=2, t=PACK)
+        pages = []
+
+        def load_pages(first, last):
+            for i in range(first, last):
+                page = sbuf([P, T2], F32, "page%d" % i)
+                nc.sync.dma_start(out=page[:], in_=page_rows[i // PACK, i % PACK])
+                pages.append(page)
+
+        wgs_dealt = [load_wgs(0, nc.gpsimd)]
+        w3_raw.append(load_weight_columns(w3, 1, "stage0"))
+        load_pages(0, 1)
+        w1_raw.append(load_weight_columns(w1, 1, "stage1"))
         idx3 = load_list(offs3, "idx3")
-        load_page(1)
-        wgs_dealt.append(load_wgs(1, [nc.sync] * 4))
-        load_page(2)
-        load_page(3)
+        load_pages(1, 2)
+        wgs_dealt.append(load_wgs(1, nc.sync))
+        load_pages(2, 4)
         gs_col = sbuf([P, 2, PACK], F32, "gs_col")
         nc.sync.dma_start(out=gs_col[:], in_=gs.rearrange("(a p t) -> p a t", a=2, t=PACK))
         idx4 = load_list(offs4, "idx4")
-        load_page(4)
-        w4_rows = w4.rearrange("(a p j) n -> a p j n", a=2, j=PACK)
+        load_pages(4, 5)
         w4_first = sbuf([P, PACK, H], F32, "tab")
-        nc.sync.dma_start(out=w4_first[:], in_=w4_rows[0])
+        nc.sync.dma_start(out=w4_first[:], in_=w4[0:HALF, :].rearrange("(p j) n -> p j n", j=PACK))
         w4_raw = [w4_first[:, :, 0:HALF], w4_first[:, :, HALF:H]]
-        load_page(5)
-        load_page(6)
-        load_page(7)
+        load_pages(5, TILES)
 
         w5_codes = sbuf([P, 2, 2 * H], U8, "w5_codes")
         w5_plane = sbuf([P, 2, H], U8, "w5_plane")
         for a in range(2):
-            deal(w5_codes[:, a, :], w5_raw[:, a, :], w5_plane[:, a, :], w5_plane_raw[:, a, :])
+            deal_packed(w5_codes[:, a, :], w5_raw[:, a, :], w5_plane[:, a, :], w5_plane_raw[:, a, :])
 
-        def transpose_sum(dst, first, second):
-            for jb in range(4):
-                cols = slice(jb * P, (jb + 1) * P)
-                nc.tensor.matmul(dst[:, cols], first[jb], ident[:], start=True, stop=False, is_transpose=True)
-                nc.tensor.matmul(dst[:, cols], second[jb], ident[:], start=False, stop=True, is_transpose=True)
-
-        def blocks(tile):
-            return [tile[:, jb * P : (jb + 1) * P] for jb in range(4)]
-
-        def reduce_angle(n, a, jh, t):
+        def reduce_angle(a, t, half):
             cols = slice(t * P, (t + 1) * P)
+            blocks = [slice(c * P, (c + 1) * P) for c in range(HALF // P)]
             d = bank("d")
-            for jb in range(4):
-                js = slice(jb * P, (jb + 1) * P)
+            for block in blocks:
                 nc.tensor.matmul_mx(
-                    d[:, js], lhsT=v_codes[jh][:, js].bitcast(FP8X4), lhsT_scale=v_plane[jh][:, js],
+                    d[:, block], lhsT=v_codes[half][:, block].bitcast(FP8X4), lhsT_scale=v_plane[half][:, block],
                     rhs=w3_codes[a][:, cols].bitcast(FP8X4), rhs_scale=w3_plane[a][:, cols], start=True, stop=True,
                 )
             turns = sbuf([P, HALF], F32, "turns", 2)
             nc.scalar.activation(turns[:], d[:], ACT.Copy, scale=1.0 / (2.0 * math.pi))
             whole = sbuf([P, HALF], U32, "whole", 2)
-            if True:
-                nc.scalar.activation(whole[:], turns[:], ACT.Copy, bias=ROUNDER)
-            else:
-                nc.gpsimd.tensor_scalar(whole[:].bitcast(I32), turns[:], 1.0, ROUNDER, MULT, ADD)
+            nc.scalar.activation(whole[:], turns[:], ACT.Copy, bias=ROUNDER)
             minus_whole = sbuf([P, HALF], F32, "minus_whole", 2)
             nc.scalar.activation(minus_whole[:], whole[:], ACT.Copy, scale=-1.0, bias=ROUNDER)
             part = bank("part")
-            transpose_sum(part, blocks(minus_whole), blocks(turns))
-            return part, whole
+            for block in blocks:
+                nc.tensor.matmul(part[:, block], minus_whole[:, block], ident[:], start=True, stop=False, is_transpose=True)
+                nc.tensor.matmul(part[:, block], turns[:, block], ident[:], start=False, stop=True, is_transpose=True)
+            return part
 
-        def sine(part, sin_d):
-            nc.scalar.activation(sin_d, part[:], ACT.Sin, bias=zero[:], scale=2.0 * math.pi)
-
-        def tanh_and_f(n, a, jh, t):
+        def unit_terms(n, a, t, half):
+            part = reduce_angle(a, t, half)
             b, f = bank("b"), bank("f")
-            cols = slice(t * P, (t + 1) * P)
+            first = a * HALF + t * P
             nc.tensor.matmul_mx(
-                b[:], lhsT=w2_codes[:, a * H + 2 * t * P : a * H + 2 * (t + 1) * P].bitcast(FP4X4),
-                lhsT_scale=w2_plane[:, a * HALF + t * P : a * HALF + (t + 1) * P],
-                rhs=v_codes[jh][:].bitcast(FP8X4), rhs_scale=v_plane[jh][:], start=True, stop=True,
+                b[:], lhsT=w2_codes[:, 2 * first : 2 * (first + P)].bitcast(FP4X4),
+                lhsT_scale=w2_plane[:, first : first + P],
+                rhs=v_codes[half][:].bitcast(FP8X4), rhs_scale=v_plane[half][:], start=True, stop=True,
             )
             tanh_b = sbuf([P, HALF], F32, "tanh_b", 3)
             nc.scalar.activation(tanh_b[:], b[:], ACT.Tanh, bias=zero[:])
+            cols = slice(t * P, (t + 1) * P)
             nc.tensor.matmul_mx(
                 f[:], lhsT=w1_codes[a][:, cols].bitcast(FP8X4), lhsT_scale=w1_plane[a][:, cols],
-                rhs=v_codes[jh][:].bitcast(FP8X4), rhs_scale=v_plane[jh][:], start=True, stop=True,
+                rhs=v_codes[half][:].bitcast(FP8X4), rhs_scale=v_plane[half][:], start=True, stop=True,
             )
-            if n < 0:
-                return tanh_b, f
-            f_sb = sbuf([P, HALF], F32, "f_sb", 3)
-            nc.scalar.copy(f_sb[:], f[:])
-            return tanh_b, f_sb
+            if n >= UNITS_ON_VECTOR:
+                f_sb = sbuf([P, HALF], F32, "psum_copy", 3)
+                nc.scalar.copy(f_sb[:], f[:])
+                f = f_sb
+            sin_d = sbuf([P, HALF], F32, "sin_d", 3)
+            nc.scalar.activation(sin_d[:], part[:], ACT.Sin, bias=zero[:], scale=2.0 * math.pi)
+            return sin_d, tanh_b, f
 
-        def place(n, a, jh, t, sin_d, tanh_b, f):
-            prod = sbuf([P, HALF], F32, "prod", 2)
-            (nc.vector if n < 0 else nc.gpsimd).tensor_tensor(prod[:], tanh_b[:], sin_d[:], MULT)
-            (nc.vector if n < 0 else nc.gpsimd).tensor_tensor(prod[:], f[:], prod[:], ADD)
-            window = pages[a * PACK + t][:].indirect(idx2[:, jh * 32 : (jh + 1) * 32])
-            weights = wgs_dealt[t // 2][:, t % 2, jh * HALF : (jh + 1) * HALF]
-            if n < 0:
-                nc.vector.tensor_tensor(window, prod[:], weights, MULT)
-            else:
-                new = sbuf([P, HALF], F32, "new", 3)
-                nc.gpsimd.tensor_tensor(new[:], prod[:], weights, MULT)
-                nc.vector.tensor_copy(window, new[:])
-
-        w4_codes = [sbuf([P, H], U32, "w4_codes%d" % a) for a in range(2)]
-        w4_plane = [sbuf([P, H], U8, "w4_plane%d" % a) for a in range(2)]
-
-        def quantize_w4(a, b):
-            cols = slice(b * HALF, (b + 1) * HALF)
-            quantize_dealt("SSSS"[2 * a + b], w4_raw[2 * a + b], w4_codes[a][:, cols], w4_plane[a][:, cols])
+        def place(n, a, t, half, sin_d, tanh_b, f):
+            engine = nc.vector if n < UNITS_ON_VECTOR else nc.gpsimd
+            h = sbuf([P, HALF], F32, "h", 2)
+            engine.tensor_tensor(h[:], tanh_b[:], sin_d[:], MULT)
+            engine.tensor_tensor(h[:], f[:], h[:], ADD)
+            new = sbuf([P, HALF], F32, "new", 3)
+            engine.tensor_tensor(new[:], h[:], wgs_dealt[t // 2][:, t % 2, half * HALF : (half + 1) * HALF], MULT)
+            entries = idx2[:, half * LIST_COLS : (half + 1) * LIST_COLS]
+            nc.vector.tensor_copy(pages[a * PACK + t][:].indirect(entries), new[:])
 
         x_codes, x_plane = [], []
 
-        def fetch_x(a, t, xs):
-            nc.vector.tensor_copy(xs[:, t, :], pages[a * PACK + t][:].indirect(idx3[:]))
-
-        def quantize_x(a, xs, late):
-            nc.scalar.copy(late[:, 0:PACK], gs_col[:, a, :])
+        def quantize_x(a, xs, spent):
+            nc.scalar.copy(spent[:, 0:PACK], gs_col[:, a, :])
             for t in range(PACK):
-                nc.scalar.activation(xs[:, t, :], xs[:, t, :], ACT.Copy, scale=late[:, t : t + 1])
-            codes = sbuf([P, 2, M], U32, "tab_plane" if a == 0 else "x_codes1")
+                nc.scalar.activation(xs[:, t, :], xs[:, t, :], ACT.Copy, scale=spent[:, t : t + 1])
+            codes = sbuf([P, 2, M], U32, "x_codes%d" % a)
             plane = sbuf([P, 2, M], U8, "x_plane%d" % a)
             src = xs[:].rearrange("p t (c i) -> p c t i", i=4)
-            for s, func in enumerate((ACT.Copy, ACT.Square)):
-                grouped = sbuf([P, PACK * M], BF16, "grouped", 4)
+            for square in range(2):
+                grouped = grouped_tile()
                 dst = grouped[:].rearrange("p (c i t) -> p c t i", i=4, t=PACK)
-                if s == 0 and "SS"[a] == "G":
-                    nc.gpsimd.tensor_scalar(dst, src, 1.0, 0.0, MULT, ADD)
-                elif s == 0 and "SS"[a] == "V":
-                    nc.vector.tensor_copy(out=dst, in_=src)
+                if square:
+                    nc.scalar.activation(dst, src, ACT.Square)
+                elif a == 0:
+                    nc.scalar.activation(dst, src, ACT.Copy)
                 else:
-                    nc.scalar.activation(dst, src, func)
-                nc.vector.quantize_mx(out=codes[:, s, :].bitcast(FP8X4), scales=plane[:, s, :], in_=grouped[:])
+                    nc.gpsimd.tensor_scalar(
+                        grouped[:].rearrange("p (m t) -> p m t", t=PACK), xs[:].rearrange("p t m -> p m t"),
+                        1.0, 0.0, MULT, ADD,
+                    )
+                nc.vector.quantize_mx(out=codes[:, square, :].bitcast(FP8X4), scales=plane[:, square, :], in_=grouped[:])
             x_codes.append(codes)
             x_plane.append(plane)
 
-        units = [(a, jh, t) for a in range(2) for t in range(PACK) for jh in range(2)]
-        fronts, angles, sines = {}, {}, {}
-        xs = [None, None]
+        units = [(a, t, half) for a in range(2) for t in range(PACK) for half in range(2)]
+        terms, xs = [], []
         for n in range(len(units) + 1):
-            if n == 5:
-                quantize_dealt("V", w3_raw[1][:], w3_codes[1][:], w3_plane[1][:])
-                quantize_dealt("S", w1_raw[1][:], w1_codes[1][:], w1_plane[1][:])
-            if n == 5:
-                for b in range(2):
-                    raw = sbuf([P, PACK, HALF], F32, "stage%d" % b)
-                    nc.sync.dma_start(out=raw[:], in_=w4_rows[1][:, :, b * HALF : (b + 1) * HALF])
-                    w4_raw.append(raw[:])
+            if n == SECOND_HALVES_AT:
+                quantize_dealt(nc.vector.tensor_copy, w3_raw[1][:], w3_codes[1][:], w3_plane[1][:])
+                quantize_dealt(nc.scalar.copy, w1_raw[1][:], w1_codes[1][:], w1_plane[1][:])
+                w4_raw.extend(load_weight_columns(w4[HALF:H, :], b, "stage%d" % b)[:] for b in range(2))
             if n < len(units):
-                part, whole = reduce_angle(n, *units[n])
-                fronts[n] = tanh_and_f(n, *units[n])
-                sines[n] = sbuf([P, HALF], F32, "sin_d", 3)
-                sine(part, sines[n][:])
-            m = n - 1
-            if m >= 0:
-                a, jh, t = units[m]
-                place(m, a, jh, t, sines[m], *fronts[m])
-                if jh == 1:
+                terms.append(unit_terms(n, *units[n]))
+            if n > 0:
+                a, t, half = units[n - 1]
+                place(n - 1, a, t, half, *terms[n - 1])
+                if half == 1:
                     if t == 0:
-                        xs[a] = sbuf([P, PACK, M], F32, "xs%d" % a)
-                    fetch_x(a, t, xs[a])
-                if m == 9:
-                    quantize_x(0, xs[0], sines[9])
+                        xs.append(sbuf([P, PACK, M], F32, "xs%d" % a))
+                    nc.vector.tensor_copy(xs[a][:, t, :], pages[a * PACK + t][:].indirect(idx3[:]))
+                if n - 1 == FIRST_X_AFTER:
+                    quantize_x(0, xs[0], terms[n - 1][0])
 
-        quantize_w4(0, 0)
-        quantize_w4(0, 1)
-        quantize_w4(1, 0)
-        quantize_w4(1, 1)
-        quantize_x(1, xs[1], sines[15])
+        w4_codes = [sbuf([P, H], U32, "w4_codes%d" % a) for a in range(2)]
+        w4_plane = [sbuf([P, H], U8, "w4_plane%d" % a) for a in range(2)]
+        for a in range(2):
+            for b in range(2):
+                cols = slice(b * HALF, (b + 1) * HALF)
+                quantize_dealt(nc.scalar.copy, w4_raw[2 * a + b], w4_codes[a][:, cols], w4_plane[a][:, cols])
+        quantize_x(1, xs[1], terms[-1][0])
+
+        ys = [bank(tag) for tag in ("d", "b", "part", "f") for twice in range(2)]
+        for a in range(2):
+            for i in range(TILES):
+                cols = slice(i * P, (i + 1) * P)
+                nc.tensor.matmul_mx(
+                    ys[i][:], lhsT=w4_codes[a][:, cols].bitcast(FP8X4), lhsT_scale=w4_plane[a][:, cols],
+                    rhs=x_codes[a][:, 0, :].bitcast(FP8X4), rhs_scale=x_plane[a][:, 0, :], start=(a == 0), stop=False,
+                )
+                nc.tensor.matmul_mx(
+                    ys[i][:], lhsT=w5_codes[:, a, 2 * i * P : 2 * (i + 1) * P].bitcast(FP4X4), lhsT_scale=w5_plane[:, a, cols],
+                    rhs=x_codes[a][:, 1, :].bitcast(FP8X4), rhs_scale=x_plane[a][:, 1, :], start=False, stop=(a == 1),
+                )
 
         inlet = [sbuf([P, PACK, M], F32, tag) for tag in ("stage1", "xs1")]
-        out_rows = out.rearrange("(a p t) m -> a t p m", a=2, t=PACK)
-        ys = [bank(tag) for tag in ("d", "d", "b", "b", "part", "part", "f", "f")]
-        for a in range(2):
-            for i in range(8):
-                for s in range(2):
-                    cols = slice(i * P, (i + 1) * P)
-                    if s == 0:
-                        lhs, lhs_scale = w4_codes[a][:, cols].bitcast(FP8X4), w4_plane[a][:, cols]
-                    else:
-                        lhs, lhs_scale = w5_codes[:, a, 2 * i * P : 2 * (i + 1) * P].bitcast(FP4X4), w5_plane[:, a, cols]
-                    nc.tensor.matmul_mx(
-                        ys[i][:], lhsT=lhs, lhsT_scale=lhs_scale,
-                        rhs=x_codes[a][:, s, :].bitcast(FP8X4), rhs_scale=x_plane[a][:, s, :],
-                        start=(a == 0 and s == 0), stop=(a == 1 and s == 1),
-                    )
-        for i in range(8):
+        for i in range(TILES):
             nc.vector.tensor_copy(inlet[i // PACK][:, i % PACK, :], pages[i][:].indirect(idx4[:]))
-        for i in range(8):
-            b, t = i // PACK, i % PACK
-            nc.vector.scalar_tensor_tensor(
-                inlet[b][:, t, :], ys[i][:], gs_col[:, b, t : t + 1], inlet[b][:, t, :], MULT, MULT
-            )
-            nc.sync.dma_start(out=out_rows[b, t], in_=inlet[b][:, t, :])
+        out_rows = out.rearrange("(a p t) m -> a t p m", a=2, t=PACK)
+        for i in range(TILES):
+            a, t = divmod(i, PACK)
+            result = inlet[a][:, t, :]
+            if i < OUT_TILES_ON_GPSIMD:
+                y_scaled = sbuf([P, M], F32, "psum_copy", 3)
+                nc.scalar.activation(y_scaled[:], ys[i][:], ACT.Copy, scale=gs_col[:, a, t : t + 1])
+                nc.gpsimd.tensor_tensor(result, result, y_scaled[:], MULT)
+            else:
+                nc.vector.scalar_tensor_tensor(result, ys[i][:], gs_col[:, a, t : t + 1], result, MULT, MULT)
+            nc.sync.dma_start(out=out_rows[a, t], in_=result)

import math
from contextlib import ExitStack

import concourse.mybir as mybir
from concourse.masks import make_identity

K, H, T, S, T2, M = 512, 1024, 4096, 1024, 2048, 512
FLOPS = 2 * (3 * K * H * S + 2 * H * H * M)

F32 = mybir.dt.float32
BF16 = mybir.dt.bfloat16
I32 = mybir.dt.int32
U32 = mybir.dt.uint32
U16 = mybir.dt.uint16
U8 = mybir.dt.uint8
FP8X4 = mybir.dt.float8_e4m3fn_x4
FP4X4 = mybir.dt.float4_e2m1fn_x4
ACT = mybir.ActivationFunctionType
MULT = mybir.AluOpType.mult
ADD = mybir.AluOpType.add

P = 128
PACK = 4
HALF = P * PACK
LIST_COLS = HALF // 16
TILES = H // P
ROUNDER = 1.5 * 2.0**23
UNITS_ON_VECTOR = 1
SECOND_HALVES_AT = 5
FIRST_X_AFTER = 10
OUT_TILES_ON_GPSIMD = 3


def tile_list_digester_layer_features_kernel(
    tc, tab_words, tab_scales, offs, offs2, offs3, offs4, w1, w2_words, w2_scales, w3, wgs, page0, gs, w4,
    w5_words, w5_scales, out,
):
    nc = tc.nc
    with ExitStack() as ctx:
        lists = ctx.enter_context(tc.tile_pool(name="lists", bufs=1))
        sb = ctx.enter_context(tc.tile_pool(name="sb", bufs=1))
        psum = ctx.enter_context(tc.psum_pool(name="psum", bufs=2))

        def sbuf(shape, dtype, tag, bufs=1):
            return sb.tile(shape, dtype, name=tag, tag=tag, bufs=bufs, align_bytes=64)

        def bank(tag):
            return psum.tile([P, HALF], F32, name=tag, tag=tag)

        def load_list(src, name):
            tile = lists.tile([P, src.shape[1]], U16, name=name)
            nc.sync.dma_start(tile[:], src)
            return tile

        def load_scale_rows(plane, rows):
            for q in range(4):
                nc.sync.dma_start(
                    out=plane[32 * q : 32 * q + 4].bitcast(I32),
                    in_=rows[:, 4 * q : 4 * q + 4, :].rearrange("a r n -> r a n").bitcast(I32),
                )

        def load_weight_columns(rows, b, tag):
            raw = sbuf([P, PACK, HALF], F32, tag)
            nc.sync.dma_start(out=raw[:], in_=rows[:, b * HALF : (b + 1) * HALF].rearrange("(p j) c -> p j c", j=PACK))
            return raw

        def grouped_tile():
            return sbuf([P, PACK * HALF], BF16, "grouped", 4)

        def quantize_dealt(copy, raw, codes, plane):
            grouped = grouped_tile()
            copy(
                out=grouped[:].rearrange("p (t m j) -> p m t j", t=PACK, j=PACK),
                in_=raw.rearrange("p j (m t) -> p m t j", t=PACK),
            )
            nc.vector.quantize_mx(out=codes.bitcast(FP8X4), scales=plane, in_=grouped[:])

        def deal_packed(codes, raw, plane, plane_raw):
            nc.vector.tensor_copy(
                out=codes.bitcast(U16).rearrange("p (b t m) -> p b t m", b=2, t=PACK),
                in_=raw.bitcast(U16).rearrange("p (b m t) -> p b t m", b=2, t=PACK),
            )
            nc.vector.tensor_copy(
                out=plane.rearrange("p (b t m) -> p b t m", b=2, t=PACK),
                in_=plane_raw.rearrange("p (b m t) -> p b t m", b=2, t=PACK),
            )

        tab_plane = sbuf([P, 1, T], U8, "x_codes0")
        nc.vector.memset(tab_plane[:].bitcast(I32), 0)
        w2_plane_raw = sbuf([P, 1, H], U8, "w2_plane_raw")
        nc.vector.memset(w2_plane_raw[:].bitcast(I32), 0)
        w5_plane_raw = sbuf([P, 2, H], U8, "w5_plane_raw")
        nc.vector.memset(w5_plane_raw[:].bitcast(I32), 0)
        zero_in = sbuf([P, 1], F32, "zero_in")
        nc.vector.memset(zero_in[:], 0.0)
        zero = sbuf([P, 1], F32, "zero")
        nc.scalar.activation(zero[:], zero_in[:], ACT.Silu)
        ident = sbuf([P, P], F32, "ident")
        make_identity(nc, ident[:])

        idx = load_list(offs, "idx")
        w2_raw = sbuf([P, 2 * H], U8, "w2_raw")
        nc.sync.dma_start(out=w2_raw[:].bitcast(I32), in_=w2_words[0].bitcast(I32))
        w3_raw = [load_weight_columns(w3, 0, "wgs0")]
        load_scale_rows(tab_plane, tab_scales)
        tab = sbuf([P, T], U32, "tab")
        nc.sync.dma_start(out=tab[:].bitcast(I32), in_=tab_words[0].rearrange("p n t -> p (n t)").bitcast(I32))
        load_scale_rows(w2_plane_raw, w2_scales)
        w1_raw = [load_weight_columns(w1, 0, "stage1")]
        w5_raw = sbuf([P, 2, 2 * H], U8, "xs1")
        nc.sync.dma_start(out=w5_raw[:].bitcast(I32), in_=w5_words.rearrange("a p n -> p a n").bitcast(I32))
        load_scale_rows(w5_plane_raw, w5_scales)
        idx2 = load_list(offs2, "idx2")

        w1_codes = [sbuf([P, HALF], U32, "w1_codes%d" % a) for a in range(2)]
        w1_plane = [sbuf([P, HALF], U8, "w1_plane%d" % a) for a in range(2)]
        w3_codes = [sbuf([P, HALF], U32, "w3_codes%d" % a) for a in range(2)]
        w3_plane = [sbuf([P, HALF], U8, "w3_plane%d" % a) for a in range(2)]
        w2_codes = sbuf([P, 2 * H], U8, "w2_codes")
        w2_plane = sbuf([P, H], U8, "w2_plane")
        v_codes, v_plane = [], []

        def gather_table(half):
            entries = idx[:, half * LIST_COLS : (half + 1) * LIST_COLS]
            codes = sbuf([P, HALF], U32, "v_codes%d" % half)
            nc.vector.tensor_copy(codes[:], tab[:].indirect(entries))
            plane = sbuf([P, HALF], U8, "v_plane%d" % half)
            nc.vector.tensor_copy(plane[:], tab_plane[:, 0, :].indirect(entries))
            v_codes.append(codes)
            v_plane.append(plane)

        quantize_dealt(nc.vector.tensor_copy, w3_raw[0][:], w3_codes[0][:], w3_plane[0][:])
        deal_packed(w2_codes[:], w2_raw[:], w2_plane[:], w2_plane_raw[:, 0, :])
        gather_table(0)
        quantize_dealt(nc.vector.tensor_copy, w1_raw[0][:], w1_codes[0][:], w1_plane[0][:])
        gather_table(1)

        def load_wgs(pair, queue):
            wgs_tile = sbuf([P, 2, S], F32, "wgs%d" % pair)
            wgs_rows = wgs.rearrange("(p t) j -> p t j", t=PACK)[:, 2 * pair : 2 * pair + 2, :]
            for q in range(4):
                queue.dma_start(out=wgs_tile[32 * q : 32 * q + 32], in_=wgs_rows)
            return wgs_tile

        page_rows = page0.rearrange("(a p t) c -> a t p c", a=2, t=PACK)
        pages = []

        def load_pages(first, last):
            for i in range(first, last):
                page = sbuf([P, T2], F32, "page%d" % i)
                nc.sync.dma_start(out=page[:], in_=page_rows[i // PACK, i % PACK])
                pages.append(page)

        wgs_dealt = [load_wgs(0, nc.gpsimd)]
        w3_raw.append(load_weight_columns(w3, 1, "stage0"))
        load_pages(0, 1)
        w1_raw.append(load_weight_columns(w1, 1, "stage1"))
        idx3 = load_list(offs3, "idx3")
        load_pages(1, 2)
        wgs_dealt.append(load_wgs(1, nc.sync))
        load_pages(2, 4)
        gs_col = sbuf([P, 2, PACK], F32, "gs_col")
        nc.sync.dma_start(out=gs_col[:], in_=gs.rearrange("(a p t) -> p a t", a=2, t=PACK))
        idx4 = load_list(offs4, "idx4")
        load_pages(4, 5)
        w4_first = sbuf([P, PACK, H], F32, "tab")
        nc.sync.dma_start(out=w4_first[:], in_=w4[0:HALF, :].rearrange("(p j) n -> p j n", j=PACK))
        w4_raw = [w4_first[:, :, 0:HALF], w4_first[:, :, HALF:H]]
        load_pages(5, TILES)

        w5_codes = sbuf([P, 2, 2 * H], U8, "w5_codes")
        w5_plane = sbuf([P, 2, H], U8, "w5_plane")
        for a in range(2):
            deal_packed(w5_codes[:, a, :], w5_raw[:, a, :], w5_plane[:, a, :], w5_plane_raw[:, a, :])

        def reduce_angle(a, t, half):
            cols = slice(t * P, (t + 1) * P)
            blocks = [slice(c * P, (c + 1) * P) for c in range(HALF // P)]
            d = bank("d")
            for block in blocks:
                nc.tensor.matmul_mx(
                    d[:, block], lhsT=v_codes[half][:, block].bitcast(FP8X4), lhsT_scale=v_plane[half][:, block],
                    rhs=w3_codes[a][:, cols].bitcast(FP8X4), rhs_scale=w3_plane[a][:, cols], start=True, stop=True,
                )
            turns = sbuf([P, HALF], F32, "turns", 2)
            nc.scalar.activation(turns[:], d[:], ACT.Copy, scale=1.0 / (2.0 * math.pi))
            whole = sbuf([P, HALF], U32, "whole", 2)
            nc.scalar.activation(whole[:], turns[:], ACT.Copy, bias=ROUNDER)
            minus_whole = sbuf([P, HALF], F32, "minus_whole", 2)
            nc.scalar.activation(minus_whole[:], whole[:], ACT.Copy, scale=-1.0, bias=ROUNDER)
            part = bank("part")
            for block in blocks:
                nc.tensor.matmul(part[:, block], minus_whole[:, block], ident[:], start=True, stop=False, is_transpose=True)
                nc.tensor.matmul(part[:, block], turns[:, block], ident[:], start=False, stop=True, is_transpose=True)
            return part

        def unit_terms(n, a, t, half):
            part = reduce_angle(a, t, half)
            b, f = bank("b"), bank("f")
            first = a * HALF + t * P
            nc.tensor.matmul_mx(
                b[:], lhsT=w2_codes[:, 2 * first : 2 * (first + P)].bitcast(FP4X4),
                lhsT_scale=w2_plane[:, first : first + P],
                rhs=v_codes[half][:].bitcast(FP8X4), rhs_scale=v_plane[half][:], start=True, stop=True,
            )
            tanh_b = sbuf([P, HALF], F32, "tanh_b", 3)
            nc.scalar.activation(tanh_b[:], b[:], ACT.Tanh, bias=zero[:])
            cols = slice(t * P, (t + 1) * P)
            nc.tensor.matmul_mx(
                f[:], lhsT=w1_codes[a][:, cols].bitcast(FP8X4), lhsT_scale=w1_plane[a][:, cols],
                rhs=v_codes[half][:].bitcast(FP8X4), rhs_scale=v_plane[half][:], start=True, stop=True,
            )
            if n >= UNITS_ON_VECTOR:
                f_sb = sbuf([P, HALF], F32, "psum_copy", 3)
                nc.scalar.copy(f_sb[:], f[:])
                f = f_sb
            sin_d = sbuf([P, HALF], F32, "sin_d", 3)
            nc.scalar.activation(sin_d[:], part[:], ACT.Sin, bias=zero[:], scale=2.0 * math.pi)
            return sin_d, tanh_b, f

        def place(n, a, t, half, sin_d, tanh_b, f):
            engine = nc.vector if n < UNITS_ON_VECTOR else nc.gpsimd
            h = sbuf([P, HALF], F32, "h", 2)
            engine.tensor_tensor(h[:], tanh_b[:], sin_d[:], MULT)
            engine.tensor_tensor(h[:], f[:], h[:], ADD)
            new = sbuf([P, HALF], F32, "new", 3)
            engine.tensor_tensor(new[:], h[:], wgs_dealt[t // 2][:, t % 2, half * HALF : (half + 1) * HALF], MULT)
            entries = idx2[:, half * LIST_COLS : (half + 1) * LIST_COLS]
            nc.vector.tensor_copy(pages[a * PACK + t][:].indirect(entries), new[:])

        x_codes, x_plane = [], []

        def quantize_x(a, xs, spent):
            nc.scalar.copy(spent[:, 0:PACK], gs_col[:, a, :])
            for t in range(PACK):
                nc.scalar.activation(xs[:, t, :], xs[:, t, :], ACT.Copy, scale=spent[:, t : t + 1])
            codes = sbuf([P, 2, M], U32, "x_codes%d" % a)
            plane = sbuf([P, 2, M], U8, "x_plane%d" % a)
            src = xs[:].rearrange("p t (c i) -> p c t i", i=4)
            for square in range(2):
                grouped = grouped_tile()
                dst = grouped[:].rearrange("p (c i t) -> p c t i", i=4, t=PACK)
                if square:
                    nc.scalar.activation(dst, src, ACT.Square)
                elif a == 0:
                    nc.scalar.activation(dst, src, ACT.Copy)
                else:
                    nc.gpsimd.tensor_scalar(
                        grouped[:].rearrange("p (m t) -> p m t", t=PACK), xs[:].rearrange("p t m -> p m t"),
                        1.0, 0.0, MULT, ADD,
                    )
                nc.vector.quantize_mx(out=codes[:, square, :].bitcast(FP8X4), scales=plane[:, square, :], in_=grouped[:])
            x_codes.append(codes)
            x_plane.append(plane)

        units = [(a, t, half) for a in range(2) for t in range(PACK) for half in range(2)]
        terms, xs = [], []
        for n in range(len(units) + 1):
            if n == SECOND_HALVES_AT:
                quantize_dealt(nc.vector.tensor_copy, w3_raw[1][:], w3_codes[1][:], w3_plane[1][:])
                quantize_dealt(nc.scalar.copy, w1_raw[1][:], w1_codes[1][:], w1_plane[1][:])
                w4_raw.extend(load_weight_columns(w4[HALF:H, :], b, "stage%d" % b)[:] for b in range(2))
            if n < len(units):
                terms.append(unit_terms(n, *units[n]))
            if n > 0:
                a, t, half = units[n - 1]
                place(n - 1, a, t, half, *terms[n - 1])
                if half == 1:
                    if t == 0:
                        xs.append(sbuf([P, PACK, M], F32, "xs%d" % a))
                    nc.vector.tensor_copy(xs[a][:, t, :], pages[a * PACK + t][:].indirect(idx3[:]))
                if n - 1 == FIRST_X_AFTER:
                    quantize_x(0, xs[0], terms[n - 1][0])

        w4_codes = [sbuf([P, H], U32, "w4_codes%d" % a) for a in range(2)]
        w4_plane = [sbuf([P, H], U8, "w4_plane%d" % a) for a in range(2)]
        for a in range(2):
            for b in range(2):
                cols = slice(b * HALF, (b + 1) * HALF)
                quantize_dealt(nc.scalar.copy, w4_raw[2 * a + b], w4_codes[a][:, cols], w4_plane[a][:, cols])
        quantize_x(1, xs[1], terms[-1][0])

        ys = [bank(tag) for tag in ("d", "b", "part", "f") for twice in range(2)]
        for a in range(2):
            for i in range(TILES):
                cols = slice(i * P, (i + 1) * P)
                nc.tensor.matmul_mx(
                    ys[i][:], lhsT=w4_codes[a][:, cols].bitcast(FP8X4), lhsT_scale=w4_plane[a][:, cols],
                    rhs=x_codes[a][:, 0, :].bitcast(FP8X4), rhs_scale=x_plane[a][:, 0, :], start=(a == 0), stop=False,
                )
                nc.tensor.matmul_mx(
                    ys[i][:], lhsT=w5_codes[:, a, 2 * i * P : 2 * (i + 1) * P].bitcast(FP4X4), lhsT_scale=w5_plane[:, a, cols],
                    rhs=x_codes[a][:, 1, :].bitcast(FP8X4), rhs_scale=x_plane[a][:, 1, :], start=False, stop=(a == 1),
                )

        inlet = [sbuf([P, PACK, M], F32, tag) for tag in ("stage1", "xs1")]
        for i in range(TILES):
            nc.vector.tensor_copy(inlet[i // PACK][:, i % PACK, :], pages[i][:].indirect(idx4[:]))
        out_rows = out.rearrange("(a p t) m -> a t p m", a=2, t=PACK)
        for i in range(TILES):
            a, t = divmod(i, PACK)
            result = inlet[a][:, t, :]
            if i < OUT_TILES_ON_GPSIMD:
                y_scaled = sbuf([P, M], F32, "psum_copy", 3)
                nc.scalar.activation(y_scaled[:], ys[i][:], ACT.Copy, scale=gs_col[:, a, t : t + 1])
                nc.gpsimd.tensor_tensor(result, result, y_scaled[:], MULT)
            else:
                nc.vector.scalar_tensor_tensor(result, ys[i][:], gs_col[:, a, t : t + 1], result, MULT, MULT)
            nc.sync.dma_start(out=out_rows[a, t], in_=result)
